import numpy as np, ml_dtypes
CORES = [8,136,40,168]
N = 4
BF = ml_dtypes.bfloat16
W, C, K, VISITS = 2048, 512, 192, 6
LEV = np.arange(16).reshape(1, 1, 16, 1)
HC = 39 + 14 * LEV
UC = 5 + 10 * LEV
SIZES = np.array([1, 1, 2, 2, 3, 4, 6, 8, 16, 32, 64, 128, 256, 512, W, W]).reshape(1, 1, 16, 1)
def take(a, i):
    return np.take_along_axis(a, i, a.ndim - 1)
def cell(z):
    return (255 + np.add.reduce(HC * z, axis=2)) & (C - 1)
def first(keys):
    return np.unique(keys, return_index=True)[1]
def parts(rng, amp=12):
    pool = np.argsort(rng.random((8, 16, W)), axis=-1); pl = np.broadcast_to(pool[None], (N, 8, 16, W))
    fo = np.where(rng.random((N, 8, W)) < 0.6, np.arange(W), rng.integers(0, W, (N, 8, W)))
    la = take(pl, (rng.random((N, 8, 16, K)) * SIZES).astype(np.int64)); bk = take(pl, (rng.random((N, 8, 16, C)) * SIZES).astype(np.int64))
    cen = rng.integers(40, 216, (1, 8, 16, 1))
    far = rng.random((N, 8, 1, W)) < 0.06
    for q in range(N):
        for g in range(8):
            far[q, g, 0, fo[q, g, pool[g, :4, :2].reshape(-1)]] = False
    x = np.where(far, rng.integers(0, 256, (N, 8, 16, W)), cen + rng.integers(-amp, amp + 1, (N, 8, 16, W)))
    z = np.where(rng.random((N, 8, 1, K)) < 0.04, rng.integers(0, 256, (N, 8, 16, K)), cen + rng.integers(-amp, amp + 1, (N, 8, 16, K)))
    t = 235 - 4 * LEV + rng.integers(0, 4, (N, 8, 16, 1))
    c = cell(z); same = rng.random((N, 8, K)) < 0.15
    for q in range(N):
        for g in range(8):
            j = np.flatnonzero(same[q, g]); j = j[first(c[q, g, j])]
            bk[q, g][:, c[q, g, j]] = la[q, g][:, j]
    return x, fo, bk, la, z, t
def pack(x, fo, bk, la, z, t):
    return {"x": np.ascontiguousarray(x.reshape(N, 128, W)).astype(np.float32).astype(BF), "fw": np.ascontiguousarray(fo).astype(np.int32),
            "bk": np.ascontiguousarray(bk.reshape(N, 128, C)).astype(np.int32), "la": np.ascontiguousarray(la.reshape(N, 128, K)).astype(np.int32),
            "zz": np.ascontiguousarray(z.reshape(N, 128, K)).astype(np.float32).astype(BF), "th": np.ascontiguousarray(t.reshape(N, 128, 1)).astype(np.int32)}
def setup_inputs(rng):
    return pack(*parts(rng))
def setup_inputs_spread(rng):
    x = np.minimum((np.exp2(8 * rng.random((N, 8, 1, W))) * rng.random((N, 8, 16, W))).astype(np.int64), 255)
    z = np.minimum((np.exp2(8 * rng.random((N, 8, 1, K))) * rng.random((N, 8, 16, K))).astype(np.int64), 255)
    t = -np.sort(-np.minimum(np.exp2(12 * rng.random((N, 8, 16, 1))).astype(np.int64), 4080), axis=2)
    fo = rng.integers(0, W, (N, 8, W)); la = (W * rng.random((N, 8, 16, K)) ** 3).astype(np.int64); bk = (W * rng.random((N, 8, 16, C)) ** 3).astype(np.int64)
    return pack(x, fo, np.minimum(bk, W - 1), np.minimum(la, W - 1), z, t)
def setup_inputs_ends(rng):
    def both(n):
        k = rng.integers(0, 3, (N, 8, 1, n)); return np.where(k == 0, 0, np.where(k == 1, 255, 255 * rng.integers(0, 2, (N, 8, 16, n))))
    x, z = both(W), both(K)
    fo = (W - 1) * rng.integers(0, 2, (N, 8, W)); bk = (W - 1) * rng.integers(0, 2, (N, 8, 16, C)); la = (W - 1) * rng.integers(0, 2, (N, 8, 16, K))
    t = 4080 * (rng.random((N, 8, 16, 1)) < rng.choice(np.array([0.5, 0.8, 0.95]), (N, 8, 1, 1))).astype(np.int64)
    t[N - 1, 7] = 4080; t[:, 6] = 4080; t[:, 6, 15] = 0
    near = (255 * (16 - np.arange(16) // 2) - 1 + np.arange(16) % 2).reshape(16, 1)
    for g, o in ((3, 1), (5, -1)):
        z[:, g] = 255 * (np.argsort(rng.random((N, 16, K)), axis=1) < np.argsort(rng.random((N, 1, K)), axis=-1) % 17)
        t[:, g] = near[::o]
    x[:, 1::2, :, 0] = 0; x[:, 1::2, :, W - 1] = 255; fo[:, 1::2, 0] = 0; fo[:, 1::2, W - 1] = W - 1
    z[..., K - 1] = 0; la[..., K - 1] = W - 1; z[..., K - 2] = 255; la[..., K - 2] = 0
    bk[:, 1::2, :, 255] = 0; bk[:, 1::2, :, C - 1] = W - 1
    return pack(x, fo, bk, la, z, t)
def setup_inputs_corners(rng):
    x, fo, bk, la, z, t = parts(rng); a = np.arange(W)
    pat = [a, 0 * a, 0 * a + W - 1, np.maximum(a - 1, 0), W - 1 - a, (a + 1) % W, a ^ 1]
    kind = rng.integers(0, 4, (N, 8)); kind[0] = (1, 0, 2, 3, 1, 3, 0, 1)
    r = rng.random((N, 8, 1, K)); la = np.where(r < 0.1, 0, np.where(r < 0.2, W - 1, la))
    z[..., K - 1] = z[..., 0]; c = cell(z)
    for q in range(N):
        for g in range(8):
            i = (g + q) % 8
            if i < 7: fo[q, g] = pat[i]
            if kind[q, g] == 1: t[q, g] = 4080
            if kind[q, g] == 2: t[q, g] = 0
            if kind[q, g] == 3: t[q, g] = np.where(LEV[0, 0] < rng.integers(1, 16), 4080, 0)
            for j in rng.permutation(K)[:8]:
                bk[q, g][:, c[q, g, j]] = la[q, g][:, j]; bk[q, g, 15, c[q, g, j]] = rng.integers(0, W)
    return pack(x, fo, bk, la, z, t)
def setup_inputs_crowd(rng):
    x, fo, bk, la, z, t = parts(rng)
    for q in range(N):
        for g in range(8):
            k = g % 4; j = K - 1 if q == 0 else int(rng.integers(0, K))
            if k != 3: z[q, g] = z[q, g][:, :1].copy(); la[q, g] = la[q, g][:, :1].copy()
            if k == 2: t[q, g] = 0
            else: fo[q, g] = np.arange(W); la[q, g, 0] = W - 1; t[q, g, 0] = 4080
            c = (255 + np.add.reduce(HC[0, 0] * z[q, g], axis=0)) & (C - 1)
            if k in (0, 1): bk[q, g][:, c[0]] = la[q, g][:, 0]; bk[q, g, 0, c[0]] = rng.integers(0, W - 1)
            if k == 3: bk[q, g, 0] = rng.integers(0, W - 1, C)
            if k == 1 or (k == 3 and q % 2 == 1): la[q, g][:, j] = bk[q, g][:, c[j]]
    return pack(x, fo, bk, la, z, t)
def setup_inputs_ties(rng):
    x, fo, bk, la, z, t = parts(rng, 1)
    t = -np.sort(-rng.integers(14, 25, (N, 8, 16, 1)), axis=2)
    for g in (2, 6):
        mid = rng.integers(40, 216, (16, 1)); fo[:, g] = np.arange(W)
        x[:, g] = mid + rng.integers(-1, 2, (N, 16, W)); z[:, g] = mid + rng.integers(-1, 2, (N, 16, K))
    t[:, 2] = 22 - LEV[0, 0] // 2
    for q in range(N):
        a = rng.integers(0, W - 1, (16, 1)); la[q, 2] = a; bk[q, 2] = a
        x[q, 2, :, W - 1] = x[q, 2, :, int(a[0, 0])]
        j = rng.permutation(K)[:1 + q % 3]; la[q, 2, 0, j] = W - 1; z[q, 2][:, j] = x[q, 2, :, W - 1:]
    la[:, 6] = rng.integers(0, W, (N, 16, K)); bk[:, 6] = rng.integers(0, W, (N, 16, C)); t[:, 6] = 9
    return pack(x, fo, bk, la, z, t)
def check_inputs(d):
    bad = []
    for k, hi in (("x", 255), ("fw", W - 1), ("bk", W - 1), ("la", W - 1), ("zz", 255), ("th", 4080)):
        v = np.asarray(d[k]).astype(np.float64)
        if not (np.min(v) >= 0 and np.max(v) <= hi): bad.append("range of " + k)
        elif np.any(v != np.floor(v)): bad.append("whole numbers of " + k)
    return bad
def reference(x, fw, bk, la, zz, th):
    X = x.astype(np.float32).astype(np.int32).reshape(N, 8, 16, W); Z = zz.astype(np.float32).astype(np.int32).reshape(N, 8, 16, K)
    F = fw.astype(np.int64).reshape(N, 8, W); B = bk.astype(np.int64).reshape(N, 8, 16, C); L = la.astype(np.int64).reshape(N, 8, 16, K)
    T = th.astype(np.int64).reshape(N, 8, 16, 1); A = np.zeros((N, 8, 1, 1), np.int64)
    for v in range(VISITS):
        if v > 0:
            s = 1 + (v - 1) % (N - 1); L = np.roll(L, s, axis=0); Z = np.roll(Z, s, axis=0)
        L = take(F, L.reshape(N, 8, 16 * K)).reshape(N, 8, 16, K)
        c = cell(Z)
        G = take(F, take(B, c[:, :, None, :]).reshape(N, 8, 16 * K)).reshape(N, 8, 16, K)
        d = np.add.reduce(np.abs(take(X, L.reshape(N, 8, 1, 16 * K)).reshape(N, 8, 16, 16, K) - Z[:, :, :, None, :]), axis=2)
        e = np.add.reduce(np.abs(take(X, G.reshape(N, 8, 1, 16 * K)).reshape(N, 8, 16, 16, K) - Z[:, :, :, None, :]), axis=2)
        fail = d > T + (A & 15); ks = np.where(np.any(fail, axis=2), np.argmax(fail, axis=2), 16)
        good = (G != L) & (e <= T); m = np.where(np.any(good, axis=2), np.argmax(good, axis=2), 16)
        merge = m < ks
        u = ((255 + np.add.reduce(UC * Z, axis=2)) & 1023)[:, :, None, :]
        new = np.where(LEV >= ks[:, :, None, :], (((L * u) >> 5) + L + 613 * LEV) & (W - 1), L)
        w = np.take_along_axis(new, np.minimum(ks, 15)[:, :, None, :], 2)
        val = np.where(ks[:, :, None, :] < 16, Z, (take(X, w) + Z) >> 1)
        mm = np.minimum(m, 15)[:, :, None, :]; gm = np.take_along_axis(G, mm, 2); lm = np.take_along_axis(L, mm, 2)
        hi = np.maximum(gm, lm)[:, :, 0]; lo = np.minimum(gm, lm)[:, :, 0]
        Z = np.where(m[:, :, None, :] < 16, (Z + take(X, gm)) >> 1, Z)
        for q in range(N):
            for g in range(8):
                j = first(w[q, g, 0]); X[q, g][:, w[q, g, 0, j]] = val[q, g][:, j]
                j = first(c[q, g]); B[q, g][:, c[q, g, j]] = new[q, g][:, j]
                j = np.flatnonzero(merge[q, g]); j = j[first(hi[q, g, j])]; F[q, g, hi[q, g, j]] = lo[q, g, j]
        A = np.add.reduce(merge.astype(np.int64), axis=2)[:, :, None, None]
        L = new
    return {"yx": X.reshape(N, 128, W).astype(np.float32).astype(BF), "yf": F.astype(np.float32), "yb": B.reshape(N, 128, C).astype(np.float32),
            "yl": L.reshape(N, 128, K).astype(np.float32), "yz": Z.reshape(N, 128, K).astype(np.float32).astype(BF)}

@@ -1,0 +1,494 @@
+from concourse.mybir import AluOpType as ALU, ActivationFunctionType as ACT
+
+W, C, K, NV, N = 2048, 512, 192, 6, 4
+BIG = 4096.0
+MAG = 12582912.0
+HALF = 0.5 - 1.0 / 2048
+F0, X0 = 16, 48 + W
+XZ = X0 + W
+GZ = 6
+CH = ((0, 64), (64, 128), (128, K))
+OPT = {"cl": "SSS", "cg": "SVV", "period": 27572.0}
+
+TIMES = """iYfwi:-735 iSxw:-735 iSlai:-723 iYxw:-729 iSthi:-729 iYbw:-723 iVrin:-713 iGpi:-735 iGgm:-675 iGrr:-631 iGdm:-718
+iGeoi:-289 iVpi:-658,-683 iVcol:-642,-667,-627,-617,-439,-393,-348,-607,-598,-588,375,1876,1245 iVbo:-538 iVwd:-522,-429
+iVwdhc:-2 iVbouc:-12 iVbohc:-285 iVi1:-578 iVc255:-735,-552 iVfwh:-495 iPp0:-354 iSftmp:-258,-378,-318,-198
+iVxw:-144,-276,-219,-68 iPp1:-427 iPp2:-390 iPp3:-317 iVlu:-338 iVeo:-153 iVi32:-512 iVtm4:-383 iVcnt:70 iGtm5:-333
+iGcnt:205 iVwdb:-414 iVwdn:-403 iVwd2:612 iVib:-88 iVtm1:-373,21 iVti:-315 iVtm2:837 iVtn:231 iVq2:1215 iVtm3:-78
+iVq1:1502 iVzsv:818 iVi2:-357 iVr15:-163 iVbo32:2064 iVtm0:-722 iVwy:-562,1885 Pp4:42,2103,2221 Vub1:218 Vub2:275 Vbu:329
+Vbb:364 Gzr:42,99,156,213,270,327 Vzr:151,205,81,94,55,107,68,262,351,338 Sfg:532,710,887 Pp1:722,899,1076,2396
+Vgp:978,1170,1417 Sfl:0,177,355 Pp0:189,367,600,1966,2799 Vlp:319,579,774 Vkbf:588 Veqb:1180 Pp5:1371,2006,1897,2317,2493
+Vofb:1950 Slf:1291 Sp0:1432 Vdl:402,598,790 Srdl:1064,1178,1318 Pp2:1190,1303,1450,2414 Vegl:1394 Vt1:1660 Sp1:1720
+Vmx:1759 Vmn:1782 Pp3:-243,1681,1517,1751,1880,2120,2288 Vdg:994,1218,1483 Srdg:1459 Vrdg:1427,1683 Ssg:1909 Pp7:1948,2074
+Sohm:1983 Sex:2142 Vofz:2215 Vsz:2231 Ssz2:2335 Szo:2368 GZ:2407 Nxw:2437 Ssf:1572 Pp6:1646,1664,1927,2203 Snge:1747
+Sp2:1693 Vt3:1805 Vt4:1834 Vnew:1863 Vpw:1892 Vls:2088 GL:2123 Nlu:2153 Skw:2086 Skrw:1956
+Vbw:1965,1984,2002,2020,2039,2057,2075,2269,2287,2305,2324,2342 Veqw:2111 Vsv:1927 Vofw:2408 Ssv2:2018 Sdat:2308,2492
+Sp7:2115 Vpgl:2154,2177 Shir:2233 Shiw:2300 Veqh:2354 Slo2:2426 Slo3:2459
+Vxw:2424,2442,2460,2479,2497,2519,2745,2764,2782,2800,2877,2896,2531,2550,2568,2586,2605,2623,2641,2660,2678,2696,2715,2733
+Voff:2509 Vai:2921,2937 Vnthr:2952 Pp5z:1257,2063,1897,2328 Yyz:2412 Vylf:1909 Yyl:1944 Skwz:2143 Skrwz:2079
+Vbwz:1971,1989,2007,2025,2044,2062,2080,2099,2117,2135,2285,2304 Vybf:2340 Yyb:2400 Veqwz:2194 Vsvz:1932 Vofwz:2419
+Ssv2z:2019 Sdatz:2052,2502 Veqhz:2331
+Vxwz:2434,2453,2471,2489,2508,2526,2548,2565,2585,2605,2625,2645,2560,2578,2597,2621,2640,2658,2676,2701,2719,2738,2756,2774
+Voffz:2538 Yyx:2650 Syff:2940 Syf:3006"""
+WHEN = {"%s.%d" % (x.split(":")[0], i): 10 * int(y) for x in TIMES.split() for i, y in enumerate(x.split(":")[1].split(","))}
+OWN_END = ("Vxw", "Vbw", "Vsv", "Vofw", "Veqw", "Ssv2", "Sdat", "Pp5", "Skw", "Skrw", "Veqh", "Voff")
+
+SCRATCH = {
+    "xw": ("sbuf", [128, XZ + NV * K], "bfloat16"),
+    "bw": ("sbuf", [128, 16 + C], "int32"),
+    "dat": ("sbuf", [128, 2 * K], "bfloat16"),
+    "cnt": ("sbuf", [128, 16, 144], "bfloat16"),
+}
+for _names, _n, _dt in (
+        ("lu ls", NV * K, "uint16"), ("zo", NV * K, "bfloat16"), ("fl fg dl dg rdl rdg zra zrb", 16 * K, "bfloat16"),
+        ("ub1 ub2a ub2b", 400, "int32"), ("ofba ofbb ofw off", 24, "uint16"), ("lai t4 new", K, "int32"),
+        ("thi pi ai", 4, "int32"), ("fwi", 512, "int32"), ("fwh", 512, "float16"), ("ftmp", W, "float32"),
+        ("col kw hiw", 16, "float32"), ("gm dm bo32 i32", 128, "float32"),
+        ("bo bouc bohc i1 i2 ib ti tn q1 q2 r15 tm0 tm1 tm2 tm3 tm4 tm5", 128, "bfloat16"),
+        ("wd wdhc wdb wdn wd2", 144, "bfloat16"), ("wy", 40, "bfloat16"), ("rin rr", 512, "bfloat16"),
+        ("c255", 400, "bfloat16"), ("eoi", 12, "int32"), ("eo bu ofz", 12, "uint16"), ("zsv kbf", 12, "float32"),
+        ("bb lp gp", K, "uint16"), ("eqb eqw eqh egl sf nge sg ohm ex sv sz", K, "bfloat16"),
+        ("lf t1 t3 mx mn krw hir lo2 lo3 sv2 sz2 ylf", K, "float32"), ("pw", K, "float16"), ("pgl", 2 * K, "float16"),
+        ("acc nthr", 4, "float32"), ("ybf yff", 512, "float32")):
+    for _x in _names.split():
+        SCRATCH[_x] = ("sbuf", [128, _n], _dt)
+for _b in range(8):
+    SCRATCH["p%d" % _b] = ("psum", [128, 512], "float32")
+
+DMAS = ["fw", "x", "bk", "zz", "la", "th", "yx", "yf", "yb", "yl", "yz"]
+SEMAPHORES = (["eV", "eS", "eP", "eG", "sent"] + ["d_" + n for n in DMAS]
+              + ["aL%d" % v for v in range(1, NV)] + ["aZ%d" % v for v in range(1, NV)])
+
+cA, cG, cCK, cGE, cQ1, cQ2, cHC, cUC, cCR, cT5, cNT5, cA16, cE15 = range(13)
+
+
+def R(name, lo, hi, step=1, p=None, idx=None):
+    return ("r", name, lo, hi, step, p, idx)
+
+
+def IND(win, off):
+    return ("i", win, off)
+
+
+def col(c):
+    return R("col", c, c + 1)
+
+
+def full(n):
+    return R(n, 0, SCRATCH[n][1][1])
+
+
+def psum(r):
+    return r[0] == "r" and SCRATCH[r[1]][0] == "psum"
+
+
+def regs(x):
+    if not isinstance(x, tuple):
+        return []
+    return [x[1], x[2]] if x[0] == "i" else [x]
+
+
+def build():
+    ops, names, base = [], {}, [None]
+
+    def add(eng, kind, args, wr, rd):
+        w, r = [], []
+        for x in wr:
+            if x[0] == "i":
+                w.append(x[1])
+                r.append(x[2])
+            else:
+                w.append(x)
+        for x in rd:
+            r.extend(regs(x))
+        key = eng + (w[0][1][:-1] if w[0][1][:-1] in ("zr", "ub2", "ofb") else w[0][1]) if w else eng + args[0]
+        names[key] = names.get(key, -1) + 1
+        key = "%s%s%s.%d" % ("i" if base[0] is None else "", key, "z" if names.get("last") and key in OWN_END else "", names[key])
+        ops.append({"eng": eng, "kind": kind, "args": args, "w": w, "r": r, "key": key, "base": base[0] or 0.0})
+
+    def cp(out, a):
+        add("V", "copy", (out, a), [out], [a])
+
+    def tt(out, a, b, op):
+        add("V", "tt", (out, a, b, op), [out], [a, b])
+
+    def ts(out, a, s1, o1, s2=None, o2=None):
+        add("V", "ts", (out, a, s1, s2, o1, o2), [out], [a, s1, s2])
+
+    def ms(out, c):
+        add("V", "ms", (out, c), [out], [])
+
+    def act(out, a, f, bias=0.0, scale=1.0, acc=None):
+        add("S", "act", (out, a, f, bias, scale, acc), [out] + ([acc] if acc else []), [a, bias, scale])
+
+    def mm(lst, start=True, stop=True):
+        add("P", "mm", lst, [x[0] for x in lst], [x[1] for x in lst] + [x[2] for x in lst])
+        ops[-1]["group"] = (start, stop)
+
+    def gp(kind, args, out, ins):
+        add("G", kind, args, [out], ins)
+
+    def dma(q, name, out, a):
+        add(q, "dma", (name, out, a), [out] if out[0] == "r" else [], [a] if a[0] == "r" else [])
+
+    def wrap(out, name, src, lo, hi):
+        return [(out, R(name, 15 - a, 143 - a), R(src, lo + a, hi, 16)) for a in range(16)]
+
+    def CNT(idx, n):
+        return R("cnt", 0, 2304, idx=(idx, n))
+
+    def contest(out, eq, key):
+        mm([(out, CNT((slice(None), a, slice(15 - a, 143 - a)), 128), R(eq, a, K, 16)) for a in range(1, 16)]
+           + [(out, full("i32"), key)])
+
+    def dist(out, src, j0, j1, on, adr, zr):
+        d, r = R(src, 16 * j0, 16 * j1), R("r" + src, 16 * j0, 16 * j1)
+        tt(d, IND(R("xw", X0, XZ), R(adr, j0, j1)), R(zr, 16 * j0, 16 * j1), ALU.subtract)
+        if on == "S":
+            act(r, d, ACT.Abs)
+            return wrap(out, "wd", "r" + src, 16 * j0, 16 * j1)
+        ts(r, d, 0.0, ALU.max)
+        return wrap(out, "wdn", src, 16 * j0, 16 * j1) + wrap(out, "wd2", "r" + src, 16 * j0, 16 * j1)
+
+    def scatter(win, off, src, lo):
+        for jj in range(11, -1, -1):
+            cp(IND(win, R(off, 2 * jj, 2 * jj + 1)), R(src, lo + 16 * jj, lo + 16 * jj + 16))
+
+    P32 = (0, 32)
+    dma("Y", "fw", R("fwi", 0, 512, p=P32), ("h", "fw"))
+    dma("S", "zz", R("xw", XZ, XZ + K), ("h", "zz"))
+    dma("S", "la", full("lai"), ("h", "la"))
+    dma("Y", "x", R("xw", X0, XZ), ("h", "x"))
+    dma("S", "th", R("thi", 0, 1), ("h", "th"))
+    dma("Y", "bk", R("bw", 16, 16 + C), ("h", "bk"))
+    ms(R("rin", 0, 512, p=P32), 1.0 / 16)
+    gp("iota", (R("pi", 0, 1), [[0, 1]], 0, 1), R("pi", 0, 1), [])
+    gp("iota", (full("gm"), [[1, 8], [0, 16]], 0, 0), full("gm"), [])
+    gp("aff", (R("rr", 0, 512, p=P32), R("rin", 0, 512, p=P32), [[-1, 4], [-4, 8], [0, 16]], ALU.is_equal, 0.0, 0, 1),
+       full("rr"), [full("rin")])
+    gp("iota", (full("dm"), [[1, 128]], 0, -1), full("dm"), [])
+    gp("iota", (full("eoi"), [[1, 12]], 0, 0), full("eoi"), [])
+    ts(R("pi", 1, 2), R("pi", 0, 1), 15, ALU.bitwise_and)
+    ts(R("pi", 2, 3), R("pi", 0, 1), 4, ALU.arith_shift_right)
+    cp(col(cA), R("pi", 1, 2))
+    cp(col(cG), R("pi", 2, 3))
+    for c, m, b in ((cCR, 1.0 / 16, -7.5 / 16), (cHC, 28.0, 78.0), (cUC, 10.0, 5.0), (cCK, 613.0, -0.484375),
+                    (cGE, -1.0, -1.0), (cQ2, -2.0, 0.0)):
+        ts(col(c), col(cA), m, ALU.mult, b, ALU.add)
+    ts(col(cA16), col(cA), 16.0, ALU.mult)
+    ts(col(cE15), col(cA), 15.0, ALU.is_equal)
+    tt(col(cQ1), col(cQ2), col(cE15), ALU.add)
+    ts(full("bo"), full("gm"), col(cG), ALU.is_equal)
+    ms(full("wd"), 0.0)
+    cp(R("wd", 15, 143, 16), R("bo", 0, 128, 16))
+    ts(full("wdhc"), full("wd"), col(cHC), ALU.mult)
+    ts(full("bouc"), full("bo"), col(cUC), ALU.mult)
+    ts(full("bohc"), full("bo"), col(cHC), ALU.mult)
+    ts(full("i1"), full("dm"), 0.0, ALU.is_equal)
+    ms(R("c255", 0, K), 255.0)
+    ms(R("c255", K, 400), 510.0)
+    ts(R("fwh", 0, 512, p=P32), R("fwi", 0, 512, p=P32), -float(W), ALU.add)
+    for s in range(4):
+        mm([(full("p%d" % s), R("rr", 128 * s, 128 * s + 128, p=P32), R("fwh", 0, 512, p=P32))])
+        act(R("ftmp", 512 * s, 512 * s + 512), full("p%d" % s), ACT.Identity, bias=col(cCR))
+        ts(R("xw", F0 + 512 * s, F0 + 512 + 512 * s), R("ftmp", 512 * s, 512 * s + 512), MAG, ALU.add, MAG, ALU.subtract)
+    cp(R("lu", 0, K), full("lai"))
+    cp(full("eo"), full("eoi"))
+    ts(full("i32"), full("dm"), 0.0, ALU.is_equal)
+    ms(full("tm4"), -2 * BIG)
+    ms(CNT((slice(None), slice(None), slice(None)), 2304), 0.0)
+    gp("aff", (full("tm5"), full("tm4"), [[0, 16], [-16, 8]], ALU.is_ge, 0.0, 0, 1), full("tm5"), [full("tm4")])
+    cv = CNT((slice(None), slice(None), slice(15, 143, 16)), 128)
+    gp("aff", (cv, full("tm5"), [[1, 16], [16, 8]], ALU.is_gt, 0.0, 0, -1), cv, [full("tm5")])
+    ts(col(cT5), R("thi", 0, 1), 0.5, ALU.add)
+    ts(col(cNT5), R("thi", 0, 1), -1.0, ALU.mult, -0.5, ALU.add)
+    ts(full("wdb"), full("wd"), col(cA), ALU.mult)
+    ts(full("wdn"), full("wd"), -1.0, ALU.mult)
+    ts(full("wd2"), full("wd"), 2.0, ALU.mult)
+    ts(full("ib"), full("i1"), BIG, ALU.mult)
+    ts(full("tm1"), full("dm"), 0.0, ALU.is_ge)
+    tt(full("ti"), full("tm1"), full("bo"), ALU.mult)
+    ts(full("tm2"), full("ti"), -2.0, ALU.mult)
+    ts(full("tn"), full("ti"), -1.0, ALU.mult)
+    ts(full("tm1"), full("i1"), 3.0, ALU.mult)
+    tt(full("q2"), full("tm2"), full("tm1"), ALU.add)
+    ts(full("tm3"), full("i1"), col(cE15), ALU.mult)
+    tt(full("q1"), full("q2"), full("tm3"), ALU.subtract)
+    ts(full("zsv"), full("eoi"), 256.0, ALU.mult, col(cA16), ALU.add)
+    ts(full("i2"), full("i1"), 2.0, ALU.mult)
+    ts(full("r15"), full("bo"), col(cE15), ALU.mult)
+    cp(full("bo32"), full("bo"))
+    ms(full("tm0"), 0.0)
+    ms(full("wy"), 0.0)
+    cp(R("wy", 3, 35, 4), R("bo", 0, 128, 16))
+
+    XT, FT, BT = R("xw", X0, XZ), R("xw", F0, F0 + W), R("bw", 16, 16 + C)
+    for v in range(NV):
+        last = v == NV - 1
+        z0 = XZ + v * K
+        Z = R("xw", z0, z0 + K)
+        base[0] = v * OPT["period"]
+        names.clear()
+        names["last"] = last
+        ub2, ofb, zr = "ub2" + "ab"[v % 2], "ofb" + "ab"[v % 2], "zr" + "ab"[v % 2]
+        mm([(R("p4", 0, 396), full("i1"), R("c255", 0, 396)), (R("p4", 0, K), full("bouc"), Z), (R("p4", K, 2 * K), full("bohc"), Z)]
+           + wrap(R("p4", 384, 396), "wdhc", "xw", z0, z0 + K))
+        cp(R("ub1", 0, 396), R("p4", 0, 396))
+        ts(R(ub2, 0, 396), R("ub1", 0, 396), 1023, ALU.bitwise_and)
+        ts(full("bu"), R(ub2, 384, 396), 0.5, ALU.mult)
+        cp(full("bb"), IND(BT, full("bu")))
+        for k in range(16):
+            if k < GZ:
+                gp("aff", (R(zr, k, 16 * K, 16), Z, [[0, K]], ALU.is_ge, 0.0, 0, 0), R(zr, k, 16 * K, 16), [Z])
+            else:
+                cp(R(zr, k, 16 * K, 16), Z)
+        for src, off, o0, bank, dst in (("fg", "bb", 0, "p1", "gp"), ("fl", "lu", v * K, "p0", "lp")):
+            for j0, j1 in CH:
+                act(R(src, 16 * j0, 16 * j1), IND(FT, R(off, o0 + j0, o0 + j1)), ACT.Identity)
+                mm(wrap(R(bank, j0, j1), "wd", src, 16 * j0, 16 * j1))
+                ts(R(dst, j0, j1), R(bank, j0, j1), float(W), ALU.add)
+        ts(full("kbf"), R(ub2, 384, 396), 0.5, ALU.mult)
+        tt(full("eqb"), IND(R(ub2, 384, 396), full("eo")), R(ub2, K, 2 * K), ALU.is_equal)
+        contest(R("p5", 0, 12), "eqb", full("kbf"))
+        ts(R(ofb, 0, 24, 2), R("p5", 0, 12), 16.0, ALU.add, col(cA), ALU.max)
+        act(full("lf"), R("p0", 0, K), ACT.Identity)
+        act(R("p0", K, 2 * K), full("lf"), ACT.Identity, bias=float(W))
+        for (j0, j1), on in zip(CH, OPT["cl"]):
+            mm(dist(R("p2", j0, j1), "dl", j0, j1, on, "lp", zr))
+        tt(full("egl"), R("p1", 0, K), full("lf"), ALU.is_equal)
+        tt(full("t1"), R("p0", K, 2 * K), R(ub2, 0, K), ALU.mult)
+        act(R("p1", K, 2 * K), full("t1"), ACT.Identity, bias=col(cCK), scale=1.0 / 32)
+        tt(full("mx"), R("p1", 0, K), full("lf"), ALU.max)
+        tt(full("mn"), R("p1", 0, K), full("lf"), ALU.min)
+        mm([(R("p3", 0, K), full("tm0"), R("c255", 0, K))], stop=False)
+        for (j0, j1), on in zip(CH, OPT["cg"]):
+            mm(dist(R("p3", j0, j1), "dg", j0, j1, on, "gp", zr), start=False, stop=False)
+        mm([(R("p3", 0, K), full("ib"), full("egl"))], start=False)
+        act(full("sg"), R("p3", 0, K), ACT.Sign, bias=col(cT5), scale=-1.0)
+        mm([(R("p7", 0, K), full("q2"), full("sg"))])
+        act(full("ohm"), R("p7", 0, K), ACT.Relu, bias=col(cQ2))
+        mm([(R("p4", 0, K), full("bo"), full("ohm"))])
+        mm(wrap(R("p3", 0, 12), "wdb", "ohm", 0, K) + [(R("p3", 0, 12), full("i32"), full("zsv"))])
+        act(full("ex"), R("p4", 0, K), ACT.Identity)
+        cp(full("ofz"), R("p3", 0, 12))
+        tt(full("sz"), IND(full("dg"), full("ofz")), full("ex"), ALU.mult)
+        mm([(R("p3", 0, K), full("i2"), Z), (R("p3", 0, K), full("i1"), full("sz"))])
+        act(full("sz2"), R("p3", 0, K), ACT.Identity, bias=MAG, scale=HALF)
+        act(R("zo", v * K, v * K + K), full("sz2"), ACT.Identity, bias=-MAG)
+        if last:
+            dma("Y", "yz", ("h", "yz"), R("zo", v * K, v * K + K))
+        else:
+            add("G", "send", ("Z", v), [], [R("zo", v * K, v * K + K)])
+            add("N", "arrive", "aZ%d" % (v + 1), [R("xw", z0 + K, z0 + 2 * K)], [])
+        act(full("sf"), R("p2", 0, K), ACT.Sign, bias=col(cNT5) if v == 0 else R("nthr", 0, 1))
+        mm([(R("p6", 0, K), full("ti"), full("sf"))])
+        mm([(R("p6", K, 2 * K), full("q1"), full("sf"))])
+        act(full("nge"), R("p6", 0, K), ACT.Sign, bias=col(cGE), scale=-1.0)
+        act(R("p2", K, 2 * K), R("p6", K, 2 * K), ACT.Relu, bias=col(cQ1))
+        tt(full("t3"), R("p1", K, 2 * K), full("nge"), ALU.mult)
+        tt(full("t4"), R("p0", K, 2 * K), full("t3"), ALU.subtract)
+        ts(full("new"), full("t4"), W - 1, ALU.bitwise_and)
+        tt(full("pw"), R("p2", K, 2 * K), full("new"), ALU.mult)
+        if last:
+            cp(full("ylf"), full("new"))
+            dma("Y", "yl", ("h", "yl"), full("ylf"))
+        else:
+            cp(R("ls", v * K, v * K + K), full("new"))
+            add("G", "send", ("L", v), [], [R("ls", v * K, v * K + K)])
+            add("N", "arrive", "aL%d" % (v + 1), [R("lu", (v + 1) * K, (v + 2) * K)], [])
+        mm(wrap(R("p5", 16, 28), "wd", "pw", 0, K))
+        mm([(R("p6", 0, K), full("bo"), full("pw"))])
+        act(R("kw", 0, 12), R("p5", 16, 28), ACT.Identity)
+        act(full("krw"), R("p6", 0, K), ACT.Identity)
+        scatter(full("bw"), ofb, "new", 0)
+        if last:
+            cp(full("ybf"), BT)
+            dma("Y", "yb", ("h", "yb"), full("ybf"))
+        D15 = R("dl", 15, 16 * K, 16)
+        mm([(R("p5", 128, 128 + K), full("r15"), full("nge"))])
+        tt(full("eqw"), IND(R("kw", 0, 12), full("eo")), full("krw"), ALU.is_equal)
+        tt(full("sv"), R("p5", 128, 128 + K), D15, ALU.mult)
+        contest(R("p5", 32, 44), "eqw", R("kw", 0, 12))
+        mm([(R("p0", 0, K), full("i2"), Z), (R("p0", 0, K), full("i1"), D15), (R("p0", 0, K), full("i1"), full("sv"))])
+        ts(R("ofw", 0, 24, 2), R("p5", 32, 44), 16.0, ALU.add, col(cA), ALU.max)
+        act(full("sv2"), R("p0", 0, K), ACT.Identity, bias=MAG, scale=HALF)
+        act(R("dat", K, 2 * K), full("sv2"), ACT.Identity, bias=-MAG)
+        mm([(R("p7", 0, K), full("i1"), full("ohm")), (R("p7", 0, K), full("tn"), full("sf"))])
+        act(R("p7", 0, K), R("p7", 0, K), ACT.Relu, bias=col(cGE), acc=None if last else R("acc", 0, 1))
+        tt(R("pgl", 0, K), R("p7", 0, K), full("mx"), ALU.mult)
+        tt(R("pgl", K, 2 * K), R("p7", 0, K), full("mn"), ALU.mult)
+        mm(wrap(R("p4", 400, 412), "wd", "pgl", 0, K))
+        mm([(R("p6", K, 2 * K), full("bo"), R("pgl", 0, K))])
+        act(full("hir"), R("p6", K, 2 * K), ACT.Identity)
+        act(R("hiw", 0, 12), R("p4", 400, 412), ACT.Identity)
+        mm([(R("p1", K, 2 * K), full("bo"), R("pgl", K, 2 * K))])
+        tt(full("eqh"), IND(R("hiw", 0, 12), full("eo")), full("hir"), ALU.is_equal)
+        contest(R("p2", 0, 12), "eqh", R("hiw", 0, 12))
+        act(full("lo2"), R("p1", K, 2 * K), ACT.Identity, bias=col(cCR), scale=1.0 / 16)
+        act(full("lo3"), full("lo2"), ACT.Identity, bias=MAG)
+        act(R("dat", 0, K), full("lo3"), ACT.Identity, bias=-MAG)
+        scatter(R("xw", X0 - 16, XZ), "ofw", "dat", K)
+        ts(R("off", 0, 24, 2), R("p2", 0, 12), float(F0 + W), ALU.add, col(cA), ALU.max)
+        scatter(R("xw", 0, X0 - 16), "off", "dat", 0)
+        if not last:
+            mm([(R("p5", 64, 65), full("bo32"), R("acc", 0, 1))])
+            cp(R("ai", 0, 1), R("p5", 64, 65))
+            ts(R("ai", 1, 2), R("ai", 0, 1), 15, ALU.bitwise_and)
+            ts(R("nthr", 0, 1), R("ai", 1, 2), -1.0, ALU.mult, col(cNT5), ALU.add)
+    dma("Y", "yx", ("h", "yx"), XT)
+    mm([(R("p0", 0, 512, p=P32), R("wy", 3 - s, 35 - s), R("xw", F0 + 512 * s, F0 + 512 + 512 * s)) for s in range(4)])
+    act(R("yff", 0, 512, p=P32), R("p0", 0, 512, p=P32), ACT.Identity, bias=float(W))
+    dma("S", "yf", ("h", "yf"), R("yff", 0, 512, p=P32))
+    return ops
+
+
+def meet(a, b):
+    if a[4] > 1 and a[4] == b[4] and (a[2] - b[2]) % a[4]:
+        return False
+    return a[1] == b[1] and a[2] < b[3] and b[2] < a[3]
+
+
+def depend(ops):
+    seen = {}
+    for i, o in enumerate(ops):
+        hard, soft = set(), set()
+        if o["kind"] == "arrive":
+            soft.add(i - 1)
+        else:
+            for x, isw in [(x, False) for x in o["r"]] + [(x, True) for x in o["w"]]:
+                for j, y, yw in seen.get(x[1], []):
+                    if meet(x, y) and (isw or yw):
+                        (soft if o["eng"] == "P" and ops[j]["eng"] == "P" else hard).add(j)
+        plain = [x for x in o["w"] if x[6] is None]
+        for x in set(plain):
+            if x[4] == 1 and x[5] is None and o["kind"] != "mm":
+                seen[x[1]] = [e for e in seen.get(x[1], []) if not (x[2] <= e[1][2] and e[1][3] <= x[3])]
+        for lst, isw in ((o["r"], False), (o["w"], True)):
+            for x in set(y[:5] for y in lst):
+                seen.setdefault(x[1], []).append((i, x, isw))
+        o["data"], o["soft"] = hard, soft - hard
+        o["banks"] = sorted(set(x[1] for x in o["r"] + o["w"] if psum(x)))
+    return ops
+
+
+def fixed(ops, when):
+    t = []
+    for o in ops:
+        t.append(max([o["base"] + when[o["key"]]] + [t[j] + 0.001 for j in o["data"] | o["soft"]]))
+    order = sorted(range(len(ops)), key=lambda i: (t[i], i))
+    bank = {}
+    for i in order:
+        o = ops[i]
+        o["hard"] = set(o["data"])
+        for b in o["banks"]:
+            o["hard"] |= set(j for e, j in bank.setdefault(b, {}).items() if e != o["eng"])
+            bank[b][o["eng"]] = i
+    return order
+
+
+PLAN = []
+
+
+def rank_program(g, core, T, topo):
+    rank = T.rank_of(core)
+    if rank is None:
+        return
+    if not PLAN:
+        PLAN.append(depend(build()))
+        PLAN.append(fixed(PLAN[0], WHEN))
+    ops, order = PLAN
+    Q = {"V": g.vector, "S": g.scalar, "P": g.tensor, "G": g, "Y": g.sync}
+
+    def ap(x):
+        if not isinstance(x, tuple):
+            return x
+        if x[0] == "h":
+            return T[x[1]][:]
+        if x[0] == "i":
+            return ap(x[1]).indirect(ap(x[2]))
+        if x[6] is not None:
+            return T[x[1]][x[6][0]]
+        ps = slice(None) if x[5] is None else slice(x[5][0], x[5][1])
+        return T[x[1]][ps, slice(x[2], x[3], x[4]) if x[4] != 1 else slice(x[2], x[3])]
+
+    def route(v):
+        s = 1 + v % (N - 1)
+        return T.cores[(rank + s) % N], T.cores[(rank - s) % N]
+
+    needed, pos, got = set(), {i: p for p, i in enumerate(order)}, {}
+    for i in order:
+        for e in "VSPG":
+            js = [j for j in ops[i]["hard"] if ops[j]["eng"] == e and ops[j]["kind"] != "dma"]
+            if js:
+                j = max(js, key=pos.get)
+                if pos[j] > got.get((ops[i]["eng"], e), -1):
+                    got[(ops[i]["eng"], e)] = pos[j]
+                    needed.add(j)
+    token, count, waited = {}, {e: 0 for e in "VSPG"}, {}
+    sent = 0
+    for i in order:
+        o = ops[i]
+        e, kind, a = o["eng"], o["kind"], o["args"]
+        if kind == "arrive":
+            token[i] = (a, len(topo.engines(route(int(a[2:]) - 1)[1], core)))
+            continue
+        want = {}
+        for j in o["hard"]:
+            if j in token:
+                s, c = token[j]
+                want[s] = max(want.get(s, 0), c)
+        q = Q[e]
+        for s in sorted(want):
+            if waited.get((e, s), 0) < want[s]:
+                q.wait_ge(T.sem[s], want[s])
+                waited[(e, s)] = want[s]
+        if kind == "dma":
+            q.dma_start(ap(a[1]), ap(a[2])).then_inc(T.sem["d_" + a[0]], 16)
+            token[i] = ("d_" + a[0], 16)
+            continue
+        if kind == "send":
+            v = a[1]
+            dst = route(v)[0]
+            rid, pid = topo.addr(dst, core)
+            if a[0] == "L":
+                src, out = T.ls[:, v * K:v * K + K], T.lu[:, (v + 1) * K:(v + 2) * K]
+            else:
+                src, out = T.zo[:, v * K:v * K + K], T.xw[:, XZ + (v + 1) * K:XZ + (v + 2) * K]
+            g.remote_dma(out, src, T.sem["a%s%d" % (a[0], v + 1)], T.sem.sent, pid, rid, topo.mask(core, dst))
+            sent += len(topo.engines(core, dst))
+            continue
+        if kind == "copy":
+            ins = q.tensor_copy(ap(a[0]), ap(a[1]))
+        elif kind == "tt":
+            ins = q.tensor_tensor(ap(a[0]), ap(a[1]), ap(a[2]), a[3])
+        elif kind == "ts":
+            if a[5] is None:
+                ins = q.tensor_scalar(ap(a[0]), ap(a[1]), ap(a[2]), None, a[4])
+            else:
+                ins = q.tensor_scalar(ap(a[0]), ap(a[1]), ap(a[2]), ap(a[3]), a[4], a[5])
+        elif kind == "ms":
+            ins = q.memset(ap(a[0]), a[1])
+        elif kind == "act":
+            ins = q.activation(ap(a[0]), ap(a[1]), a[2], bias=ap(a[3]), scale=ap(a[4]), accum_out=ap(a[5]))
+        elif kind == "mm":
+            begun = []
+            for m, (out, l, r) in enumerate(a):
+                first = o["group"][0] and not any(meet(out, y) for y in begun)
+                begun.append(out)
+                ins = q.matmul(ap(out), ap(l), ap(r), first, o["group"][1] and m == len(a) - 1)
+        elif kind == "iota":
+            if SCRATCH[a[0][1]][2] == "int32":
+                ins = q.iota(ap(a[0]), a[1], a[2], a[3])
+            else:
+                ins = q.iota(ap(a[0]), a[1], a[2], a[3], allow_small_or_imprecise_dtypes=True)
+        else:
+            ins = q.affine_select(ap(a[0]), ap(a[1]), a[2], a[3], a[4], a[5], a[6])
+        if i in needed:
+            count[e] += 1
+            ins.then_inc(T.sem["e" + e], 1)
+            token[i] = ("e" + e, count[e])
+    for e in "VSPG":
+        g.sync.wait_ge(T.sem["e" + e], count[e])
+    for n in DMAS:
+        g.sync.wait_ge(T.sem["d_" + n], 16)
+    g.wait_ge(T.sem.sent, sent)

@@ -4,51 +4,50 @@ W, C, K, NV, N = 2048, 512, 192, 6, 4
 BIG = 4096.0
 MAG = 12582912.0
 HALF = 0.5 - 1.0 / 2048
-F0, X0 = 16, 48 + W
+F0, X0 = 32, 64 + W
 XZ = X0 + W
-GZ = 6
+GZ = 5
 CH = ((0, 64), (64, 128), (128, K))
-OPT = {"cl": "SSS", "cg": "SVV", "period": 27572.0}
+OPT = {"cl": "SSS", "cg": "SVV", "period": 26788.0}
 
-TIMES = """iYfwi:-735 iSxw:-735 iSlai:-723 iYxw:-729 iSthi:-729 iYbw:-723 iVrin:-713 iGpi:-735 iGgm:-675 iGrr:-631 iGdm:-718
-iGeoi:-289 iVpi:-658,-683 iVcol:-642,-667,-627,-617,-439,-393,-348,-607,-598,-588,375,1876,1245 iVbo:-538 iVwd:-522,-429
-iVwdhc:-2 iVbouc:-12 iVbohc:-285 iVi1:-578 iVc255:-735,-552 iVfwh:-495 iPp0:-354 iSftmp:-258,-378,-318,-198
-iVxw:-144,-276,-219,-68 iPp1:-427 iPp2:-390 iPp3:-317 iVlu:-338 iVeo:-153 iVi32:-512 iVtm4:-383 iVcnt:70 iGtm5:-333
-iGcnt:205 iVwdb:-414 iVwdn:-403 iVwd2:612 iVib:-88 iVtm1:-373,21 iVti:-315 iVtm2:837 iVtn:231 iVq2:1215 iVtm3:-78
-iVq1:1502 iVzsv:818 iVi2:-357 iVr15:-163 iVbo32:2064 iVtm0:-722 iVwy:-562,1885 Pp4:42,2103,2221 Vub1:218 Vub2:275 Vbu:329
-Vbb:364 Gzr:42,99,156,213,270,327 Vzr:151,205,81,94,55,107,68,262,351,338 Sfg:532,710,887 Pp1:722,899,1076,2396
-Vgp:978,1170,1417 Sfl:0,177,355 Pp0:189,367,600,1966,2799 Vlp:319,579,774 Vkbf:588 Veqb:1180 Pp5:1371,2006,1897,2317,2493
-Vofb:1950 Slf:1291 Sp0:1432 Vdl:402,598,790 Srdl:1064,1178,1318 Pp2:1190,1303,1450,2414 Vegl:1394 Vt1:1660 Sp1:1720
-Vmx:1759 Vmn:1782 Pp3:-243,1681,1517,1751,1880,2120,2288 Vdg:994,1218,1483 Srdg:1459 Vrdg:1427,1683 Ssg:1909 Pp7:1948,2074
-Sohm:1983 Sex:2142 Vofz:2215 Vsz:2231 Ssz2:2335 Szo:2368 GZ:2407 Nxw:2437 Ssf:1572 Pp6:1646,1664,1927,2203 Snge:1747
-Sp2:1693 Vt3:1805 Vt4:1834 Vnew:1863 Vpw:1892 Vls:2088 GL:2123 Nlu:2153 Skw:2086 Skrw:1956
-Vbw:1965,1984,2002,2020,2039,2057,2075,2269,2287,2305,2324,2342 Veqw:2111 Vsv:1927 Vofw:2408 Ssv2:2018 Sdat:2308,2492
-Sp7:2115 Vpgl:2154,2177 Shir:2233 Shiw:2300 Veqh:2354 Slo2:2426 Slo3:2459
-Vxw:2424,2442,2460,2479,2497,2519,2745,2764,2782,2800,2877,2896,2531,2550,2568,2586,2605,2623,2641,2660,2678,2696,2715,2733
-Voff:2509 Vai:2921,2937 Vnthr:2952 Pp5z:1257,2063,1897,2328 Yyz:2412 Vylf:1909 Yyl:1944 Skwz:2143 Skrwz:2079
-Vbwz:1971,1989,2007,2025,2044,2062,2080,2099,2117,2135,2285,2304 Vybf:2340 Yyb:2400 Veqwz:2194 Vsvz:1932 Vofwz:2419
-Ssv2z:2019 Sdatz:2052,2502 Veqhz:2331
-Vxwz:2434,2453,2471,2489,2508,2526,2548,2565,2585,2605,2625,2645,2560,2578,2597,2621,2640,2658,2676,2701,2719,2738,2756,2774
-Voffz:2538 Yyx:2650 Syff:2940 Syf:3006"""
-WHEN = {"%s.%d" % (x.split(":")[0], i): 10 * int(y) for x in TIMES.split() for i, y in enumerate(x.split(":")[1].split(","))}
+ORDER = """iYfwi:-692 iSxw:-688 iSlai:-692 iYxw:-686 iSthi:-680 iYbw:-680 iVrin:-690 iGpi:-692 iGgm:-680 iGrr:-670 iGdm:-609
+iGeoi:-500 iVpi:-630,-620 iVcol:-611,-601,-591,-582,-572,-562,-553,-543,-533,-524,212,1434,1443,2280 iVbo:-514 iVwd:-500,-490
+iVwdhc:-480 iVbouc:-475 iVbohc:-468 iVi1:-460 iVc255:-682,-670 iVfwh:-495 iPp0:-379 iSftmp:-330,-270,-210,-150
+iVxw:-247,-181,-124,-68 iPp1:-342 iPp2:-306 iPp3:-269 iVlu:-391 iVeo:512 iVi32:-263 iVtm4:-660 iVcnt:714 iGtm5:-400
+iGcnt:849 iVwdb:1300 iVwdn:700 iVwd2:710 iVib:1070 iVtm1:-380,1310 iVti:-368 iVtm2:1320 iVq2:1330 iVtm3:1340 iVq1:1350
+iVzsv:1524 iVi2:1360 iVr15:1370 iVbo32:2132 iVtm0:-669 iVwy:1818,2300 Pp4:-21,1949,2078 Vub1:155 Vub2:206 Vbu:256 Vbb:275
+Gzr:-21,36,207,150,93 Vzr:-12,1,14,27,40,53,66,130,117,92,79 Sfg:532,823,1114 Pp1:722,1012,1303,2174 Vgp:889,1113,1383
+Sfl:0,177,355 Pp0:189,367,544,1879,2663 Vlp:313,505,697 Vkbf:265 Veqb:899 Pp5:1080,1810,2340 Vofb:1305 Slf:1518 Sp0:1551
+Vdl:329,521,713 Srdl:710,1000,1291 Pp2:835,1159,1506,2261 Vegl:1575 Vt1:1621 Sp1:1735 Vmx:1598 Vmn:1700
+Pp3:-446,1573,1371,1438,1658,1726,1793,1966,2145 Vdg:937,1129,1398 Srdg:1405 Vrdg:1315,1644 Ssg:1822 Pp7:1861,2049
+Sohm:1891 Sex:1988 Vofz:2061 Vsz:2077 Ssz2:2194 Szo:2227 GZ:2266 Nxw:2296 Ssf:1585 Pp6:1641,1828,1920 Snge:1670 Sp2:1858
+Vt3:1774 Vt4:1803 Vnew:1863 Vpgl:1959,2005,2028 Vls:1982 GL:2017 Nlu:2047
+Vbw:1892,1910,1929,1947,2114,2133,2151,2249,2267,2285,2784,2822 Vsv:1840 Ssv2:1932 Sdat:2167,2320 Sp6:1961 Shir:2090
+Shiw:2157 Veqh:2179 Voff:2352,2361 Slo2:2254 Slo3:2287 Vxw:2377,2402,2426,2451,2476,2500,2525,2550,2574,2599,2623,2648
+Sacc:2373,2387,2400 Snthr:2380,2413 Pp5z:1080,1810 Yyz:2266 Vylf:2163 Yyl:2272
+Vbwz:1892,1910,1929,1947,1965,2001,2114,2133,2151,2256,2275,2293 Vybf:2311 Yyb:2380 Vsvz:1840 Ssv2z:1932 Sdatz:2167,2320
+Veqhz:2186 Vofwz:2368 Voffz:2377 Yyx:2749 Syff:2804 Syf:2870
+Vxwz:2387,2411,2436,2461,2485,2510,2571,2651,2669,2688,2706,2724,2399,2424,2448,2473,2498,2522,2541,2559,2584,2602,2620,2639"""
+WHEN = {"%s.%d" % (x.split(":")[0], i): 10 * int(y) for x in ORDER.split() for i, y in enumerate(x.split(":")[1].split(","))}
 OWN_END = ("Vxw", "Vbw", "Vsv", "Vofw", "Veqw", "Ssv2", "Sdat", "Pp5", "Skw", "Skrw", "Veqh", "Voff")
 
 SCRATCH = {
     "xw": ("sbuf", [128, XZ + NV * K], "bfloat16"),
     "bw": ("sbuf", [128, 16 + C], "int32"),
-    "dat": ("sbuf", [128, 2 * K], "bfloat16"),
+    "dat": ("sbuf", [128, 12, 32], "bfloat16"),
     "cnt": ("sbuf", [128, 16, 144], "bfloat16"),
 }
 for _names, _n, _dt in (
         ("lu ls", NV * K, "uint16"), ("zo", NV * K, "bfloat16"), ("fl fg dl dg rdl rdg zra zrb", 16 * K, "bfloat16"),
         ("ub1 ub2a ub2b", 400, "int32"), ("ofba ofbb ofw off", 24, "uint16"), ("lai t4 new", K, "int32"),
         ("thi pi ai", 4, "int32"), ("fwi", 512, "int32"), ("fwh", 512, "float16"), ("ftmp", W, "float32"),
-        ("col kw hiw", 16, "float32"), ("gm dm bo32 i32", 128, "float32"),
+        ("col", 16, "float32"), ("gm dm bo32 i32", 128, "float32"),
         ("bo bouc bohc i1 i2 ib ti tn q1 q2 r15 tm0 tm1 tm2 tm3 tm4 tm5", 128, "bfloat16"),
         ("wd wdhc wdb wdn wd2", 144, "bfloat16"), ("wy", 40, "bfloat16"), ("rin rr", 512, "bfloat16"),
-        ("c255", 400, "bfloat16"), ("eoi", 12, "int32"), ("eo bu ofz", 12, "uint16"), ("zsv kbf", 12, "float32"),
-        ("bb lp gp", K, "uint16"), ("eqb eqw eqh egl sf nge sg ohm ex sv sz", K, "bfloat16"),
-        ("lf t1 t3 mx mn krw hir lo2 lo3 sv2 sz2 ylf", K, "float32"), ("pw", K, "float16"), ("pgl", 2 * K, "float16"),
+        ("c255", 400, "bfloat16"), ("eoi", 24, "int32"), ("eo", 24, "uint16"), ("bu ofz", 12, "uint16"), ("zsv kbf", 12, "float32"),
+        ("bb lp gp", K, "uint16"), ("eqb egl sf nge sg ohm ex sv sz", K, "bfloat16"), ("eqh", 2 * K, "bfloat16"),
+        ("lf t1 t3 mx mn lo2 lo3 sv2 sz2 ylf", K, "float32"), ("hir", 2 * K, "float32"), ("pgl", 3 * K, "float16"),
+        ("hiw", 24, "float32"),
         ("acc nthr", 4, "float32"), ("ybf yff", 512, "float32")):
     for _x in _names.split():
         SCRATCH[_x] = ("sbuf", [128, _n], _dt)
@@ -59,7 +58,7 @@ DMAS = ["fw", "x", "bk", "zz", "la", "th", "yx", "yf", "yb", "yl", "yz"]
 SEMAPHORES = (["eV", "eS", "eP", "eG", "sent"] + ["d_" + n for n in DMAS]
               + ["aL%d" % v for v in range(1, NV)] + ["aZ%d" % v for v in range(1, NV)])
 
-cA, cG, cCK, cGE, cQ1, cQ2, cHC, cUC, cCR, cT5, cNT5, cA16, cE15 = range(13)
+cA, cG, cCK, cGE, cQ1, cQ2, cHC, cUC, cCR, cT5, cNT5, cA16, cE15, cAX = range(14)
 
 
 def R(name, lo, hi, step=1, p=None, idx=None):
@@ -138,7 +137,7 @@ def build():
         return R("cnt", 0, 2304, idx=(idx, n))
 
     def contest(out, eq, key):
-        mm([(out, CNT((slice(None), a, slice(15 - a, 143 - a)), 128), R(eq, a, K, 16)) for a in range(1, 16)]
+        mm([(out, CNT((slice(None), a, slice(15 - a, 143 - a)), 128), R(eq, a, SCRATCH[eq][1][1], 16)) for a in range(1, 16)]
            + [(out, full("i32"), key)])
 
     def dist(out, src, j0, j1, on, adr, zr):
@@ -148,7 +147,14 @@ def build():
             act(r, d, ACT.Abs)
             return wrap(out, "wd", "r" + src, 16 * j0, 16 * j1)
         ts(r, d, 0.0, ALU.max)
-        return wrap(out, "wdn", src, 16 * j0, 16 * j1) + wrap(out, "wd2", "r" + src, 16 * j0, 16 * j1)
+        mm(wrap(out, "wdn", src, 16 * j0, 16 * j1), start=False, stop=False)
+        return wrap(out, "wd2", "r" + src, 16 * j0, 16 * j1)
+
+    def DAT(t):
+        return R("dat", t, t + 1, idx=((slice(None), slice(None), slice(16 * t, 16 * t + 16)), K))
+
+    def DJ(jj, t0, t1):
+        return R("dat", t0, t1, idx=((slice(None), jj, slice(16 * t0, 16 * t1)), 16 * (t1 - t0)))
 
     def scatter(win, off, src, lo):
         for jj in range(11, -1, -1):
@@ -167,7 +173,7 @@ def build():
     gp("aff", (R("rr", 0, 512, p=P32), R("rin", 0, 512, p=P32), [[-1, 4], [-4, 8], [0, 16]], ALU.is_equal, 0.0, 0, 1),
        full("rr"), [full("rin")])
     gp("iota", (full("dm"), [[1, 128]], 0, -1), full("dm"), [])
-    gp("iota", (full("eoi"), [[1, 12]], 0, 0), full("eoi"), [])
+    gp("iota", (full("eoi"), [[1, 24]], 0, 0), full("eoi"), [])
     ts(R("pi", 1, 2), R("pi", 0, 1), 15, ALU.bitwise_and)
     ts(R("pi", 2, 3), R("pi", 0, 1), 4, ALU.arith_shift_right)
     cp(col(cA), R("pi", 1, 2))
@@ -202,6 +208,7 @@ def build():
     gp("aff", (cv, full("tm5"), [[1, 16], [16, 8]], ALU.is_gt, 0.0, 0, -1), cv, [full("tm5")])
     ts(col(cT5), R("thi", 0, 1), 0.5, ALU.add)
     ts(col(cNT5), R("thi", 0, 1), -1.0, ALU.mult, -0.5, ALU.add)
+    ts(col(cAX), col(cA), 16.0, ALU.add)
     ts(full("wdb"), full("wd"), col(cA), ALU.mult)
     ts(full("wdn"), full("wd"), -1.0, ALU.mult)
     ts(full("wd2"), full("wd"), 2.0, ALU.mult)
@@ -209,12 +216,11 @@ def build():
     ts(full("tm1"), full("dm"), 0.0, ALU.is_ge)
     tt(full("ti"), full("tm1"), full("bo"), ALU.mult)
     ts(full("tm2"), full("ti"), -2.0, ALU.mult)
-    ts(full("tn"), full("ti"), -1.0, ALU.mult)
     ts(full("tm1"), full("i1"), 3.0, ALU.mult)
     tt(full("q2"), full("tm2"), full("tm1"), ALU.add)
     ts(full("tm3"), full("i1"), col(cE15), ALU.mult)
     tt(full("q1"), full("q2"), full("tm3"), ALU.subtract)
-    ts(full("zsv"), full("eoi"), 256.0, ALU.mult, col(cA16), ALU.add)
+    ts(full("zsv"), R("eoi", 0, 12), 256.0, ALU.mult, col(cA16), ALU.add)
     ts(full("i2"), full("i1"), 2.0, ALU.mult)
     ts(full("r15"), full("bo"), col(cE15), ALU.mult)
     cp(full("bo32"), full("bo"))
@@ -248,7 +254,7 @@ def build():
                 mm(wrap(R(bank, j0, j1), "wd", src, 16 * j0, 16 * j1))
                 ts(R(dst, j0, j1), R(bank, j0, j1), float(W), ALU.add)
         ts(full("kbf"), R(ub2, 384, 396), 0.5, ALU.mult)
-        tt(full("eqb"), IND(R(ub2, 384, 396), full("eo")), R(ub2, K, 2 * K), ALU.is_equal)
+        tt(full("eqb"), IND(R(ub2, 384, 396), R("eo", 0, 12)), R(ub2, K, 2 * K), ALU.is_equal)
         contest(R("p5", 0, 12), "eqb", full("kbf"))
         ts(R(ofb, 0, 24, 2), R("p5", 0, 12), 16.0, ALU.add, col(cA), ALU.max)
         act(full("lf"), R("p0", 0, K), ACT.Identity)
@@ -288,7 +294,7 @@ def build():
         tt(full("t3"), R("p1", K, 2 * K), full("nge"), ALU.mult)
         tt(full("t4"), R("p0", K, 2 * K), full("t3"), ALU.subtract)
         ts(full("new"), full("t4"), W - 1, ALU.bitwise_and)
-        tt(full("pw"), R("p2", K, 2 * K), full("new"), ALU.mult)
+        tt(R("pgl", 0, K), R("p2", K, 2 * K), full("new"), ALU.mult)
         if last:
             cp(full("ylf"), full("new"))
             dma("Y", "yl", ("h", "yl"), full("ylf"))
@@ -296,45 +302,50 @@ def build():
             cp(R("ls", v * K, v * K + K), full("new"))
             add("G", "send", ("L", v), [], [R("ls", v * K, v * K + K)])
             add("N", "arrive", "aL%d" % (v + 1), [R("lu", (v + 1) * K, (v + 2) * K)], [])
-        mm(wrap(R("p5", 16, 28), "wd", "pw", 0, K))
-        mm([(R("p6", 0, K), full("bo"), full("pw"))])
-        act(R("kw", 0, 12), R("p5", 16, 28), ACT.Identity)
-        act(full("krw"), R("p6", 0, K), ACT.Identity)
         scatter(full("bw"), ofb, "new", 0)
         if last:
             cp(full("ybf"), BT)
             dma("Y", "yb", ("h", "yb"), full("ybf"))
         D15 = R("dl", 15, 16 * K, 16)
         mm([(R("p5", 128, 128 + K), full("r15"), full("nge"))])
-        tt(full("eqw"), IND(R("kw", 0, 12), full("eo")), full("krw"), ALU.is_equal)
         tt(full("sv"), R("p5", 128, 128 + K), D15, ALU.mult)
-        contest(R("p5", 32, 44), "eqw", R("kw", 0, 12))
         mm([(R("p0", 0, K), full("i2"), Z), (R("p0", 0, K), full("i1"), D15), (R("p0", 0, K), full("i1"), full("sv"))])
-        ts(R("ofw", 0, 24, 2), R("p5", 32, 44), 16.0, ALU.add, col(cA), ALU.max)
         act(full("sv2"), R("p0", 0, K), ACT.Identity, bias=MAG, scale=HALF)
-        act(R("dat", K, 2 * K), full("sv2"), ACT.Identity, bias=-MAG)
-        mm([(R("p7", 0, K), full("i1"), full("ohm")), (R("p7", 0, K), full("tn"), full("sf"))])
-        act(R("p7", 0, K), R("p7", 0, K), ACT.Relu, bias=col(cGE), acc=None if last else R("acc", 0, 1))
-        tt(R("pgl", 0, K), R("p7", 0, K), full("mx"), ALU.mult)
-        tt(R("pgl", K, 2 * K), R("p7", 0, K), full("mn"), ALU.mult)
-        mm(wrap(R("p4", 400, 412), "wd", "pgl", 0, K))
-        mm([(R("p6", K, 2 * K), full("bo"), R("pgl", 0, K))])
-        act(full("hir"), R("p6", K, 2 * K), ACT.Identity)
-        act(R("hiw", 0, 12), R("p4", 400, 412), ACT.Identity)
-        mm([(R("p1", K, 2 * K), full("bo"), R("pgl", K, 2 * K))])
-        tt(full("eqh"), IND(R("hiw", 0, 12), full("eo")), full("hir"), ALU.is_equal)
-        contest(R("p2", 0, 12), "eqh", R("hiw", 0, 12))
+        act(DAT(1), full("sv2"), ACT.Identity, bias=-MAG)
+        mm([(R("p6", 0, K), full("i2"), full("nge")), (R("p6", 0, K), full("q2"), full("sg"))])
+        act(R("p6", 0, K), R("p6", 0, K), ACT.Relu, bias=col(cQ2), acc=None if last else R("acc", 0, 1))
+        tt(R("pgl", K, 2 * K), R("p6", 0, K), full("mx"), ALU.mult)
+        tt(R("pgl", 2 * K, 3 * K), R("p6", 0, K), full("mn"), ALU.mult)
+        mm([(R("p7", 0, 2 * K), full("bo"), R("pgl", 0, 2 * K))])
+        mm(wrap(R("p4", 400, 424), "wd", "pgl", 0, 2 * K))
+        act(full("hir"), R("p7", 0, 2 * K), ACT.Identity)
+        act(full("hiw"), R("p4", 400, 424), ACT.Identity)
+        mm([(R("p1", K, 2 * K), full("bo"), R("pgl", 2 * K, 3 * K))])
+        tt(full("eqh"), IND(full("hiw"), full("eo")), full("hir"), ALU.is_equal)
+        contest(R("p2", 0, 24), "eqh", full("hiw"))
+        if last:
+            ts(R("ofw", 0, 24, 2), R("p2", 0, 12), 16.0, ALU.add, col(cA), ALU.max)
+        else:
+            ts(R("off", 1, 24, 2), R("p2", 0, 12), float(X0), ALU.add, col(cAX), ALU.max)
         act(full("lo2"), R("p1", K, 2 * K), ACT.Identity, bias=col(cCR), scale=1.0 / 16)
         act(full("lo3"), full("lo2"), ACT.Identity, bias=MAG)
-        act(R("dat", 0, K), full("lo3"), ACT.Identity, bias=-MAG)
-        scatter(R("xw", X0 - 16, XZ), "ofw", "dat", K)
-        ts(R("off", 0, 24, 2), R("p2", 0, 12), float(F0 + W), ALU.add, col(cA), ALU.max)
-        scatter(R("xw", 0, X0 - 16), "off", "dat", 0)
+        act(DAT(0), full("lo3"), ACT.Identity, bias=-MAG)
+        if last:
+            for jj in range(11, -1, -1):
+                cp(IND(R("xw", X0 - 16, XZ), R("ofw", 2 * jj, 2 * jj + 1)), DJ(jj, 1, 2))
+        ts(R("off", 0, 24, 2), R("p2", 12, 24), float(F0 + W), ALU.add, col(cA), ALU.max)
+        for jj in range(11, -1, -1):
+            if last:
+                cp(IND(R("xw", 0, X0 - 16), R("off", 2 * jj, 2 * jj + 1)), DJ(jj, 0, 1))
+            else:
+                cp(IND(R("xw", 0, XZ), R("off", 2 * jj, 2 * jj + 2)), DJ(jj, 0, 2))
         if not last:
             mm([(R("p5", 64, 65), full("bo32"), R("acc", 0, 1))])
-            cp(R("ai", 0, 1), R("p5", 64, 65))
-            ts(R("ai", 1, 2), R("ai", 0, 1), 15, ALU.bitwise_and)
-            ts(R("nthr", 0, 1), R("ai", 1, 2), -1.0, ALU.mult, col(cNT5), ALU.add)
+            act(R("acc", 1, 2), R("p5", 64, 65), ACT.Identity, bias=-7.5 / 16, scale=1.0 / 16)
+            act(R("acc", 2, 3), R("acc", 1, 2), ACT.Identity, bias=MAG)
+            act(R("acc", 3, 4), R("acc", 2, 3), ACT.Identity, bias=-16 * MAG, scale=16.0)
+            act(R("nthr", 1, 2), R("p5", 64, 65), ACT.Identity, bias=col(cNT5), scale=-1.0)
+            act(R("nthr", 0, 1), R("nthr", 1, 2), ACT.Identity, bias=R("acc", 3, 4))
     dma("Y", "yx", ("h", "yx"), XT)
     mm([(R("p0", 0, 512, p=P32), R("wy", 3 - s, 35 - s), R("xw", F0 + 512 * s, F0 + 512 + 512 * s)) for s in range(4)])
     act(R("yff", 0, 512, p=P32), R("p0", 0, 512, p=P32), ACT.Identity, bias=float(W))

@@ -1,54 +1,62 @@
+import numpy as np
 from concourse.mybir import AluOpType as ALU, ActivationFunctionType as ACT
 
 W, C, K, NV, N = 2048, 512, 192, 6, 4
-BIG = 4096.0
 MAG = 12582912.0
 HALF = 0.5 - 1.0 / 2048
-F0, X0 = 32, 64 + W
-XZ = X0 + W
-GZ = 5
-CH = ((0, 64), (64, 128), (128, K))
-OPT = {"cl": "SSS", "cg": "SVV", "period": 26788.0}
+H = 2.0 ** 21
+KS = 12 * 17
+F0, X0 = 32, 48 + W
+XE = X0 + W
+PIECES = ((128, K), (64, 128), (0, 64))
+OPT = {"gz": 7,
+       "fv": 32,
+       "al": "SVS"}
 
-ORDER = """iYfwi:-692 iSxw:-688 iSlai:-692 iYxw:-686 iSthi:-680 iYbw:-680 iVrin:-690 iGpi:-692 iGgm:-680 iGrr:-670 iGdm:-609
-iGeoi:-500 iVpi:-630,-620 iVcol:-611,-601,-591,-582,-572,-562,-553,-543,-533,-524,212,1434,1443,2280 iVbo:-514 iVwd:-500,-490
-iVwdhc:-480 iVbouc:-475 iVbohc:-468 iVi1:-460 iVc255:-682,-670 iVfwh:-495 iPp0:-379 iSftmp:-330,-270,-210,-150
-iVxw:-247,-181,-124,-68 iPp1:-342 iPp2:-306 iPp3:-269 iVlu:-391 iVeo:512 iVi32:-263 iVtm4:-660 iVcnt:714 iGtm5:-400
-iGcnt:849 iVwdb:1300 iVwdn:700 iVwd2:710 iVib:1070 iVtm1:-380,1310 iVti:-368 iVtm2:1320 iVq2:1330 iVtm3:1340 iVq1:1350
-iVzsv:1524 iVi2:1360 iVr15:1370 iVbo32:2132 iVtm0:-669 iVwy:1818,2300 Pp4:-21,1949,2078 Vub1:155 Vub2:206 Vbu:256 Vbb:275
-Gzr:-21,36,207,150,93 Vzr:-12,1,14,27,40,53,66,130,117,92,79 Sfg:532,823,1114 Pp1:722,1012,1303,2174 Vgp:889,1113,1383
-Sfl:0,177,355 Pp0:189,367,544,1879,2663 Vlp:313,505,697 Vkbf:265 Veqb:899 Pp5:1080,1810,2340 Vofb:1305 Slf:1518 Sp0:1551
-Vdl:329,521,713 Srdl:710,1000,1291 Pp2:835,1159,1506,2261 Vegl:1575 Vt1:1621 Sp1:1735 Vmx:1598 Vmn:1700
-Pp3:-446,1573,1371,1438,1658,1726,1793,1966,2145 Vdg:937,1129,1398 Srdg:1405 Vrdg:1315,1644 Ssg:1822 Pp7:1861,2049
-Sohm:1891 Sex:1988 Vofz:2061 Vsz:2077 Ssz2:2194 Szo:2227 GZ:2266 Nxw:2296 Ssf:1585 Pp6:1641,1828,1920 Snge:1670 Sp2:1858
-Vt3:1774 Vt4:1803 Vnew:1863 Vpgl:1959,2005,2028 Vls:1982 GL:2017 Nlu:2047
-Vbw:1892,1910,1929,1947,2114,2133,2151,2249,2267,2285,2784,2822 Vsv:1840 Ssv2:1932 Sdat:2167,2320 Sp6:1961 Shir:2090
-Shiw:2157 Veqh:2179 Voff:2352,2361 Slo2:2254 Slo3:2287 Vxw:2377,2402,2426,2451,2476,2500,2525,2550,2574,2599,2623,2648
-Sacc:2373,2387,2400 Snthr:2380,2413 Pp5z:1080,1810 Yyz:2266 Vylf:2163 Yyl:2272
-Vbwz:1892,1910,1929,1947,1965,2001,2114,2133,2151,2256,2275,2293 Vybf:2311 Yyb:2380 Vsvz:1840 Ssv2z:1932 Sdatz:2167,2320
-Veqhz:2186 Vofwz:2368 Voffz:2377 Yyx:2749 Syff:2804 Syf:2870
-Vxwz:2387,2411,2436,2461,2485,2510,2571,2651,2669,2688,2706,2724,2399,2424,2448,2473,2498,2522,2541,2559,2584,2602,2620,2639"""
-WHEN = {"%s.%d" % (x.split(":")[0], i): 10 * int(y) for x in ORDER.split() for i, y in enumerate(x.split(":")[1].split(","))}
-OWN_END = ("Vxw", "Vbw", "Vsv", "Vofw", "Veqw", "Ssv2", "Sdat", "Pp5", "Skw", "Skrw", "Veqh", "Voff")
+ORDER = """iGdsel Vbb Sfl.2 Vdl Sfg iStib Pp0.1 Pp4 Vlp.1 Vdl.1 Vrdl Slg iSwdn iSi32 Slf Pp0.2 Sfg.2 Pp1 Vegl iVc1025 Vlp.2 Vgq
+Pp2.1 Vt1 Vgp Vdl.2 Sfg.1 Pp1.2 Vdg Srdl Pp1.1 Srdl.1 Srdg Pp2 Vegl.1 iVcbig Vegl.2 Vgq.1 Vgq.2 Vgp.1 Vgp.2 Vdg.1 Pp2.2 Ssf
+iScol.5 Pp3.1 Vdg.2 iVtm2 Pp6 Pp4.1 Srp Srdg.1 Sgl Srdg.2 Pp3.2 Pp6.1 Pp5.2 iGdm+ iGpi+ iGgm+ iGlvl+ iGpos+ iSzb+ iVc255+
+iYfwi+ iSthi+ iVones.1+ iVpi.1+ iVtm1+ iVpi+ iVones+ iSlai+ iVcol+ iVwd+ iYbki+ iYxw+ Vt4 iVq1 iVi1+ iVc255.1+ iVc32+ iVbo+
+iVcol.1+ iVcol.2+ iVc1k+ iVrdg+ iVcol.3+ iVtm3+ iVq2+ Sp2 Nlu Pp3.3 Pp5.1 Pp4.2 iSbo32 Sz2 Vnew iVpz Vls iVfl iVfg iVdg
+iVcbig.1 Vsv Vsvz Vpgl Vylf Vsz Vofz Vgl Sgl.1 iVcol.4+ iVwd.1+ iVcol.7+ iScol.1+ iSr15+ iGrr+ Pp1.3 Pp7 Vzo Vzs Nzb Gzr.3+
+Gzr.5+ Gzr.2+ Gzr.4+ Gzr.6+ Gzr+ Gzr.1+ GL iGsel+ GZ Vkx.1 Vkxz.1 Yyl Yyz Yyx Yyb Sd1x iSd1x iSd1f Ssv2 Vnb Vnbz Vlm Vlo16 Vkf
+Vmg Vhi0 Vd1x iVcol.8 Vd1f iVfwh+ Ssv2z Sdatz Sdx Sdxz Vsx Vsxz Vofb Vofbz Pp6.2 Pp6.3 Pp4.3 Sdf Sdfz Vsq Vsqz Vofw Vofwz Voff
+Voffz Sdat Vxw Vxwz Sjunk Vxwz.1 Sdat.1 Sdatz.1 Sbwz Sbwz.1 Sbwz.2 Sbwz.3 Sbwz.4 Sbwz.5 Sbwz.6 Sbwz.7 Sbwz.8 Sbwz.9 Sbwz.10
+Sbwz.11 Vxwz.2 Vxwz.3 Vxwz.4 Vxwz.12 Vxwz.5 Vxwz.13 Vxwz.6 Sbw Vxwz.14 Vxwz.7 Pp5.3 Vxwz.15 Snthr Vxwz.8 Sbw.1 Vxwz.16 Sa16
+Vxwz.9 Vxwz.17 Sbw.2 Vxwz.10 Sbw.6 Vxwz.18 Sbw.7 Vxwz.11 Vxwz.19 Sbw.8 Vybf Sbw.9 Vxwz.20 Sbw.3 Vxwz.21 Snthr.1 Vxwz.22 iVthi+
+Vxwz.23 iScol.4+ iVcol.6+ iVlu+ iVq2.1+ Vxw.12 iVwduc+ Vzr.1+ Pp2.3 Syff Syf Vxw.13 iVcol.9+ iVcol.5+ iPp2+ iPp7+ Pp5+ Pp3+
+iPp6+ iPp4+ Sbw.10 Vxw.1 Vxw.14 Vzr.4+ Vxw.15 Vxw.2 Vxw.16 Vxw.3 Vxw.17 iScol.6+ iSpz+ iSboh+ iSwdh+ iScol+ iScol.2+
+iSwd2+ iSxw.1+ iScol.3+ iSi2+ iSxw+ Vxw.4 Vxw.18 Sbw.4 Vxw.5 Vxw.19 Vxw.6 Vxw.20 Vxw.7 Vxw.21 iVwdhc+ iVxw+ Vzr.7+ iVxw.1+
+iVcol.10+ iVxw.2+ Vxw.22 Vxw.8 Vxw.23 iVbw+ Vxw.9 iVttl+ Vuw+ Sbw.5 Sbw.11 Sfl+ iSd1x.1+ Sfl.1+ Vfl+ Vua+ Pp0+ Vzr.2+ Vbu+
+Vkx+ Vkxz+ Vxw.10 Vzr.5+ Vxw.11 Vzr+ iVttl.1+ iVc1025.1+ Vzr.3+ Vzr.6+ Vlp+ Vzr.8+ iVtth+ iVti+""".split()
+WHEN = {x.strip("+-") + ("" if "." in x else ".0"): i / len(ORDER) - x.count("+") + x.count("-") for i, x in enumerate(ORDER)}
+OWN_END = "Vxw Sbw Vsx Vofb Vofw Vnb Sdx Ssv2 Sdat Vsv Vkx Vsq Voff Sdf".split()
+ON_SCALAR = "wdh wdn wd2 boh i32 tib pz i2 r15 d1x d1f bo32".split()
 
 SCRATCH = {
-    "xw": ("sbuf", [128, XZ + NV * K], "bfloat16"),
-    "bw": ("sbuf", [128, 16 + C], "int32"),
+    "xw": ("sbuf", [128, XE + 16], "bfloat16"),
+    "bw": ("sbuf", [128, 16 + C], "float32"),
     "dat": ("sbuf", [128, 12, 32], "bfloat16"),
-    "cnt": ("sbuf", [128, 16, 144], "bfloat16"),
+    "sel": ("sbuf", [128, 16, 128], "bfloat16"),
+    "dsel": ("sbuf", [128, 15, 128], "bfloat16"),
+    "rdg": ("sbuf", [128, 12, 16, 17], "bfloat16"),
 }
+for _x in "pos lvl".split():
+    SCRATCH[_x] = ("sbuf", [128, 12, 17], "float32")
 for _names, _n, _dt in (
-        ("lu ls", NV * K, "uint16"), ("zo", NV * K, "bfloat16"), ("fl fg dl dg rdl rdg zra zrb", 16 * K, "bfloat16"),
-        ("ub1 ub2a ub2b", 400, "int32"), ("ofba ofbb ofw off", 24, "uint16"), ("lai t4 new", K, "int32"),
-        ("thi pi ai", 4, "int32"), ("fwi", 512, "int32"), ("fwh", 512, "float16"), ("ftmp", W, "float32"),
-        ("col", 16, "float32"), ("gm dm bo32 i32", 128, "float32"),
-        ("bo bouc bohc i1 i2 ib ti tn q1 q2 r15 tm0 tm1 tm2 tm3 tm4 tm5", 128, "bfloat16"),
-        ("wd wdhc wdb wdn wd2", 144, "bfloat16"), ("wy", 40, "bfloat16"), ("rin rr", 512, "bfloat16"),
-        ("c255", 400, "bfloat16"), ("eoi", 24, "int32"), ("eo", 24, "uint16"), ("bu ofz", 12, "uint16"), ("zsv kbf", 12, "float32"),
-        ("bb lp gp", K, "uint16"), ("eqb egl sf nge sg ohm ex sv sz", K, "bfloat16"), ("eqh", 2 * K, "bfloat16"),
-        ("lf t1 t3 mx mn lo2 lo3 sv2 sz2 ylf", K, "float32"), ("hir", 2 * K, "float32"), ("pgl", 3 * K, "float16"),
-        ("hiw", 24, "float32"),
-        ("acc nthr", 4, "float32"), ("ybf yff", 512, "float32")):
+        ("lu ls", NV * K, "uint16"), ("zb zo", NV * K, "bfloat16"), ("ones", W, "bfloat16"),
+        ("fl fg dg", 16 * K + 16, "bfloat16"), ("dl rdl zra zrb", 16 * K, "bfloat16"),
+        ("uw ua", 24, "int32"), ("ofb ofw off", 24, "uint16"), ("lai t4 new", K, "int32"),
+        ("thi pi", 4, "int32"), ("fwi bki", 512, "int32"), ("fwh", 512, "float16"),
+        ("col", 24, "float32"), ("gm dm bo32 i32", 128, "float32"),
+        ("bo boh i1 i2 ti tib q1 q2 r15 tm1 tm2 tm3", 128, "bfloat16"),
+        ("wd wdhc wduc wdh wdn wd2", 144, "bfloat16"), ("rr", 512, "bfloat16"),
+        ("c255", 24, "bfloat16"), ("c1025", 36, "float16"), ("gl", 3 * K, "bfloat16"), ("bu ofz", 12, "uint16"),
+        ("tth ttl", KS, "bfloat16"), ("cbig dx", 2 * K, "bfloat16"), ("d1x sx", 2 * K, "float32"),
+        ("kx", 36, "float16"), ("kf lo16", 12, "float16"), ("mg hi0 lm junk", 12, "float32"),
+        ("bb lp gp", K, "uint16"), ("c32 c1k egl sf sv df", K, "bfloat16"), ("pgl zs", K, "float16"),
+        ("lf lg gq rp nb t1 sv2 z2 ylf d1f sq", K, "float32"), ("a16", 4, "bfloat16"), ("pz sz", KS, "float32"),
+        ("acc nthr", 4, "float32"), ("ybf", 512, "float32"), ("yff", 128, "float32")):
     for _x in _names.split():
         SCRATCH[_x] = ("sbuf", [128, _n], _dt)
 for _b in range(8):
@@ -58,11 +66,22 @@ DMAS = ["fw", "x", "bk", "zz", "la", "th", "yx", "yf", "yb", "yl", "yz"]
 SEMAPHORES = (["eV", "eS", "eP", "eG", "sent"] + ["d_" + n for n in DMAS]
               + ["aL%d" % v for v in range(1, NV)] + ["aZ%d" % v for v in range(1, NV)])
 
-cA, cG, cCK, cGE, cQ1, cQ2, cHC, cUC, cCR, cT5, cNT5, cA16, cE15, cAX = range(14)
+cA, cG, cCK, cGE, cQ1, cQ2, cHC, cUC, cF0, cF1, cNT5, cNT6, cE15, cAX, cA16, cTH, cTL = range(17)
+ALL = slice(None)
 
 
-def R(name, lo, hi, step=1, p=None, idx=None):
-    return ("r", name, lo, hi, step, p, idx)
+def S(lo, hi, step=1):
+    return slice(lo, hi, step)
+
+
+def R(name, *idx, p=None):
+    if idx and all(isinstance(i, int) for i in idx) and len(SCRATCH[name][1]) == 2:
+        idx = (slice(*idx),)
+    shape = SCRATCH[name][1][1:]
+    cols = np.arange(int(np.prod(shape))).reshape(shape)[idx].reshape(-1)
+    bits = np.zeros(int(np.prod(shape)), np.uint8)
+    bits[cols] = 1
+    return ("r", name, idx, p, int.from_bytes(np.packbits(bits).tobytes(), "big"), len(cols))
 
 
 def IND(win, off):
@@ -73,14 +92,6 @@ def col(c):
     return R("col", c, c + 1)
 
 
-def full(n):
-    return R(n, 0, SCRATCH[n][1][1])
-
-
-def psum(r):
-    return r[0] == "r" and SCRATCH[r[1]][0] == "psum"
-
-
 def regs(x):
     if not isinstance(x, tuple):
         return []
@@ -88,7 +99,7 @@ def regs(x):
 
 
 def build():
-    ops, names, base = [], {}, [None]
+    ops, names = [], {}
 
     def add(eng, kind, args, wr, rd):
         w, r = [], []
@@ -100,10 +111,12 @@ def build():
                 w.append(x)
         for x in rd:
             r.extend(regs(x))
-        key = eng + (w[0][1][:-1] if w[0][1][:-1] in ("zr", "ub2", "ofb") else w[0][1]) if w else eng + args[0]
+        key = eng + (w[0][1][:2] if w and w[0][1][:2] == "zr" else w[0][1] if w else args[0])
+        if names.get("visit") == NV - 1 and key in OWN_END:
+            key += "z"
         names[key] = names.get(key, -1) + 1
-        key = "%s%s%s.%d" % ("i" if base[0] is None else "", key, "z" if names.get("last") and key in OWN_END else "", names[key])
-        ops.append({"eng": eng, "kind": kind, "args": args, "w": w, "r": r, "key": key, "base": base[0] or 0.0})
+        ops.append({"eng": eng, "kind": kind, "args": args, "w": w, "r": r, "key": key, "nth": "%s.%d" % (key, names[key]),
+                    "visit": names.get("visit")})
 
     def cp(out, a):
         add("V", "copy", (out, a), [out], [a])
@@ -114,249 +127,268 @@ def build():
     def ts(out, a, s1, o1, s2=None, o2=None):
         add("V", "ts", (out, a, s1, s2, o1, o2), [out], [a, s1, s2])
 
+    def scan(out, a, b):
+        add("V", "scan", (out, a, b), [out], [a, b])
+
     def ms(out, c):
         add("V", "ms", (out, c), [out], [])
 
-    def act(out, a, f, bias=0.0, scale=1.0, acc=None):
+    def act(out, a, f=ACT.Identity, bias=0.0, scale=1.0, acc=None):
         add("S", "act", (out, a, f, bias, scale, acc), [out] + ([acc] if acc else []), [a, bias, scale])
 
-    def mm(lst, start=True, stop=True):
-        add("P", "mm", lst, [x[0] for x in lst], [x[1] for x in lst] + [x[2] for x in lst])
-        ops[-1]["group"] = (start, stop)
+    def lin(out, a, m, b=0.0):
+        if out[1] in ON_SCALAR:
+            act(out, a, bias=b, scale=m)
+        else:
+            ts(out, a, m, ALU.mult, b, ALU.add)
 
-    def gp(kind, args, out, ins):
-        add("G", kind, args, [out], ins)
+    def mm(lst, start=True, stop=True, each=False, after=(), group=()):
+        add("P", "mm", lst, [x[0] for x in lst] + list(group), [x[1] for x in lst] + [x[2] for x in lst] + list(after))
+        ops[-1]["group"] = (start, stop, each)
+
+    def iota(out, pat, base, cm):
+        add("G", "iota", (out, pat, base, cm), [out], [])
+
+    def aff(out, a, pat, op, fill, base, cm):
+        add("G", "aff", (out, a, pat, op, fill, base, cm), [out], [a])
 
     def dma(q, name, out, a):
         add(q, "dma", (name, out, a), [out] if out[0] == "r" else [], [a] if a[0] == "r" else [])
 
-    def wrap(out, name, src, lo, hi):
-        return [(out, R(name, 15 - a, 143 - a), R(src, lo + a, hi, 16)) for a in range(16)]
+    def wrap(out, name, part):
+        return [(out, R(name, 15 - a, 143 - a), part(a)) for a in range(16)]
 
-    def CNT(idx, n):
-        return R("cnt", 0, 2304, idx=(idx, n))
+    def every16(name, lo, hi):
+        return lambda a: R(name, lo + a, hi, 16)
 
-    def contest(out, eq, key):
-        mm([(out, CNT((slice(None), a, slice(15 - a, 143 - a)), 128), R(eq, a, SCRATCH[eq][1][1], 16)) for a in range(1, 16)]
-           + [(out, full("i32"), key)])
+    def unwrap(bank, lo, a16):
+        return [(R(bank, lo + a, lo + K, 16), R("sel", a, ALL), a16) for a in range(16)]
 
-    def dist(out, src, j0, j1, on, adr, zr):
-        d, r = R(src, 16 * j0, 16 * j1), R("r" + src, 16 * j0, 16 * j1)
-        tt(d, IND(R("xw", X0, XZ), R(adr, j0, j1)), R(zr, 16 * j0, 16 * j1), ALU.subtract)
-        if on == "S":
-            act(r, d, ACT.Abs)
-            return wrap(out, "wd", "r" + src, 16 * j0, 16 * j1)
-        ts(r, d, 0.0, ALU.max)
-        mm(wrap(out, "wdn", src, 16 * j0, 16 * j1), start=False, stop=False)
-        return wrap(out, "wd2", "r" + src, 16 * j0, 16 * j1)
+    def contest(bank, n, key):
+        return [(R(bank, s, n, 16), R("dsel", s - 1, ALL), key) for s in range(1, 16)]
 
-    def DAT(t):
-        return R("dat", t, t + 1, idx=((slice(None), slice(None), slice(16 * t, 16 * t + 16)), K))
+    def DAT(t, jj=ALL):
+        return R("dat", jj, S(16 * t, 16 * t + 16))
 
-    def DJ(jj, t0, t1):
-        return R("dat", t0, t1, idx=((slice(None), jj, slice(16 * t0, 16 * t1)), 16 * (t1 - t0)))
-
-    def scatter(win, off, src, lo):
-        for jj in range(11, -1, -1):
-            cp(IND(win, R(off, 2 * jj, 2 * jj + 1)), R(src, lo + 16 * jj, lo + 16 * jj + 16))
+    def back(name):
+        return R(name, S(KS - 1, None, -1))
 
     P32 = (0, 32)
-    dma("Y", "fw", R("fwi", 0, 512, p=P32), ("h", "fw"))
-    dma("S", "zz", R("xw", XZ, XZ + K), ("h", "zz"))
-    dma("S", "la", full("lai"), ("h", "la"))
-    dma("Y", "x", R("xw", X0, XZ), ("h", "x"))
+    dma("Y", "fw", R("fwi", p=P32), ("h", "fw"))
+    dma("S", "zz", R("zb", 0, K), ("h", "zz"))
+    dma("S", "la", R("lai"), ("h", "la"))
+    dma("Y", "x", R("xw", X0, XE), ("h", "x"))
     dma("S", "th", R("thi", 0, 1), ("h", "th"))
-    dma("Y", "bk", R("bw", 16, 16 + C), ("h", "bk"))
-    ms(R("rin", 0, 512, p=P32), 1.0 / 16)
-    gp("iota", (R("pi", 0, 1), [[0, 1]], 0, 1), R("pi", 0, 1), [])
-    gp("iota", (full("gm"), [[1, 8], [0, 16]], 0, 0), full("gm"), [])
-    gp("aff", (R("rr", 0, 512, p=P32), R("rin", 0, 512, p=P32), [[-1, 4], [-4, 8], [0, 16]], ALU.is_equal, 0.0, 0, 1),
-       full("rr"), [full("rin")])
-    gp("iota", (full("dm"), [[1, 128]], 0, -1), full("dm"), [])
-    gp("iota", (full("eoi"), [[1, 24]], 0, 0), full("eoi"), [])
+    dma("Y", "bk", R("bki"), ("h", "bk"))
+    ts(R("bw", 16, 16 + C), R("bki"), 64.0, ALU.add)
+    ms(R("ones", 0, 512), 1.0)
+    ms(R("ones", 512, W), 1.0)
+    iota(R("pi", 0, 1), [[0, 1]], 0, 1)
+    iota(R("gm"), [[1, 8], [0, 16]], 0, 0)
+    aff(R("rr", p=P32), R("ones", 0, 512, p=P32), [[-1, 4], [-4, 8], [0, 16]], ALU.is_equal, 0.0, 0, 1)
+    iota(R("dm"), [[1, 128]], 0, -1)
+    iota(R("pos"), [[0, 12], [1, 17]], 0, 0)
+    iota(R("lvl"), [[256, 12], [1, 17]], 0, 0)
+    aff(R("sel"), R("ones"), [[-1, 16], [-16, 8], [0, 16]], ALU.is_equal, 0.0, 0, 1)
+    aff(R("dsel"), R("sel", S(0, 15), ALL), [[0, 15], [-1, 128]], ALU.not_equal, -1.0, 0, 1)
     ts(R("pi", 1, 2), R("pi", 0, 1), 15, ALU.bitwise_and)
     ts(R("pi", 2, 3), R("pi", 0, 1), 4, ALU.arith_shift_right)
-    cp(col(cA), R("pi", 1, 2))
-    cp(col(cG), R("pi", 2, 3))
-    for c, m, b in ((cCR, 1.0 / 16, -7.5 / 16), (cHC, 28.0, 78.0), (cUC, 10.0, 5.0), (cCK, 613.0, -0.484375),
-                    (cGE, -1.0, -1.0), (cQ2, -2.0, 0.0)):
-        ts(col(c), col(cA), m, ALU.mult, b, ALU.add)
-    ts(col(cA16), col(cA), 16.0, ALU.mult)
+    cp(R("col", cA, cG + 1), R("pi", 1, 3))
+    for c, m, b in ((cHC, 28.0, 78.0), (cUC, 10.0, 5.0), (cCK, 613.0, -0.484375), (cGE, -1.0, -1.0), (cQ2, -2.0, 0.0),
+                    (cAX, 1.0, X0 - 16.0), (cA16, 16.0, 0.0)):
+        act(col(c), col(cA), bias=b, scale=m)
     ts(col(cE15), col(cA), 15.0, ALU.is_equal)
+    ts(col(cF1), col(cA), 8.0, ALU.is_lt, -384.0 * 16, ALU.mult)
+    ts(col(cF0), col(cF1), col(cA), ALU.add, 1.0 / 16, ALU.mult)
+    ts(col(cF1), col(cF0), 128 - 8.5 / 16, ALU.add)
+    ts(col(cF0), col(cF0), 128 - 7.5 / 16, ALU.add)
     tt(col(cQ1), col(cQ2), col(cE15), ALU.add)
-    ts(full("bo"), full("gm"), col(cG), ALU.is_equal)
-    ms(full("wd"), 0.0)
+    ts(R("bo"), R("gm"), col(cG), ALU.is_equal)
+    ms(R("wd"), 0.0)
     cp(R("wd", 15, 143, 16), R("bo", 0, 128, 16))
-    ts(full("wdhc"), full("wd"), col(cHC), ALU.mult)
-    ts(full("bouc"), full("bo"), col(cUC), ALU.mult)
-    ts(full("bohc"), full("bo"), col(cHC), ALU.mult)
-    ts(full("i1"), full("dm"), 0.0, ALU.is_equal)
-    ms(R("c255", 0, K), 255.0)
-    ms(R("c255", K, 400), 510.0)
-    ts(R("fwh", 0, 512, p=P32), R("fwi", 0, 512, p=P32), -float(W), ALU.add)
-    for s in range(4):
-        mm([(full("p%d" % s), R("rr", 128 * s, 128 * s + 128, p=P32), R("fwh", 0, 512, p=P32))])
-        act(R("ftmp", 512 * s, 512 * s + 512), full("p%d" % s), ACT.Identity, bias=col(cCR))
-        ts(R("xw", F0 + 512 * s, F0 + 512 + 512 * s), R("ftmp", 512 * s, 512 * s + 512), MAG, ALU.add, MAG, ALU.subtract)
-    cp(R("lu", 0, K), full("lai"))
-    cp(full("eo"), full("eoi"))
-    ts(full("i32"), full("dm"), 0.0, ALU.is_equal)
-    ms(full("tm4"), -2 * BIG)
-    ms(CNT((slice(None), slice(None), slice(None)), 2304), 0.0)
-    gp("aff", (full("tm5"), full("tm4"), [[0, 16], [-16, 8]], ALU.is_ge, 0.0, 0, 1), full("tm5"), [full("tm4")])
-    cv = CNT((slice(None), slice(None), slice(15, 143, 16)), 128)
-    gp("aff", (cv, full("tm5"), [[1, 16], [16, 8]], ALU.is_gt, 0.0, 0, -1), cv, [full("tm5")])
-    ts(col(cT5), R("thi", 0, 1), 0.5, ALU.add)
+    for name, f in (("wdhc", col(cHC)), ("wduc", col(cUC)), ("wdh", H), ("wdn", -H), ("wd2", 2 * H)):
+        lin(R(name), R("wd"), f)
+    ts(R("i1"), R("dm"), 0.0, ALU.is_equal)
+    ms(R("c255", 0, 12), 510.0)
+    ms(R("c255", 12, 24), 255.0)
+    cp(R("fwh", p=P32), R("fwi", p=P32))
+    for s, bank in enumerate(("p6", "p7", "p2", "p4")):
+        mm([(R(bank), R("rr", 128 * s, 128 * s + 128, p=P32), R("fwh", p=P32))])
+        if s % 2:
+            ts(R("xw", F0 + 512 * s, F0 + 512 + 512 * s), R(bank), 1.0 / 16, ALU.mult, col(cF0), ALU.add)
+        else:
+            act(R("xw", F0 + 512 * s, F0 + 512 + 512 * s), R(bank), bias=col(cF0), scale=1.0 / 16)
+    cp(R("lu", 0, K), R("lai"))
+    for name in ("fl", "fg", "dg"):
+        ms(R(name, 16 * K, 16 * K + 16), 0.0)
+    ms(R("rdg", ALL, ALL, 16), 0.0)
+    ms(R("xw", XE, XE + 16), 8192.0)
+    ms(R("c1025", 0, 24), 1025.0)
+    ms(R("c32"), 32.0)
+    ms(R("c1k"), -1024.0)
     ts(col(cNT5), R("thi", 0, 1), -1.0, ALU.mult, -0.5, ALU.add)
-    ts(col(cAX), col(cA), 16.0, ALU.add)
-    ts(full("wdb"), full("wd"), col(cA), ALU.mult)
-    ts(full("wdn"), full("wd"), -1.0, ALU.mult)
-    ts(full("wd2"), full("wd"), 2.0, ALU.mult)
-    ts(full("ib"), full("i1"), BIG, ALU.mult)
-    ts(full("tm1"), full("dm"), 0.0, ALU.is_ge)
-    tt(full("ti"), full("tm1"), full("bo"), ALU.mult)
-    ts(full("tm2"), full("ti"), -2.0, ALU.mult)
-    ts(full("tm1"), full("i1"), 3.0, ALU.mult)
-    tt(full("q2"), full("tm2"), full("tm1"), ALU.add)
-    ts(full("tm3"), full("i1"), col(cE15), ALU.mult)
-    tt(full("q1"), full("q2"), full("tm3"), ALU.subtract)
-    ts(full("zsv"), R("eoi", 0, 12), 256.0, ALU.mult, col(cA16), ALU.add)
-    ts(full("i2"), full("i1"), 2.0, ALU.mult)
-    ts(full("r15"), full("bo"), col(cE15), ALU.mult)
-    cp(full("bo32"), full("bo"))
-    ms(full("tm0"), 0.0)
-    ms(full("wy"), 0.0)
-    cp(R("wy", 3, 35, 4), R("bo", 0, 128, 16))
+    ts(col(cNT6), R("thi", 0, 1), -1.0, ALU.mult, -0.5 - 16 * 130, ALU.add)
+    ts(R("thi", 1, 2), R("thi", 0, 1), 4080, ALU.bitwise_and)
+    ts(col(cTH), R("thi", 1, 2), -1.0, ALU.mult)
+    tt(col(cTL), col(cNT5), col(cTH), ALU.subtract)
+    ts(R("tth"), R("pos"), col(cA), ALU.is_equal, col(cTH), ALU.mult)
+    ts(R("ttl"), R("pos"), col(cA), ALU.is_equal, col(cTL), ALU.mult)
+    ms(R("ttl", 16, KS, 17), -1.0)
+    lin(R("boh"), R("bo"), H)
+    lin(R("i32"), R("i1"), 1.0)
+    lin(R("pz"), R("lvl"), 1.0, col(cA16))
+    ms(R("pz", 16, KS, 17), 16.0 * K)
+    lin(R("c1025", 24, 36), R("lvl", ALL, 16), 1.0, col(cA16))
+    POS = R("pos", ALL, S(0, 16))
+    for t, c in enumerate((cAX, cA)):
+        ts(R("cbig", K * t, K * t + K), POS, col(cA), ALU.is_gt, 4096.0, ALU.mult)
+        lin(R("d1x", K * t, K * t + K), POS, 0.0, col(c))
+    lin(R("d1f"), POS, 0.0, col(cA))
+    ts(R("tm1"), R("dm"), 0.0, ALU.is_ge)
+    tt(R("ti"), R("tm1"), R("bo"), ALU.mult)
+    lin(R("tm2"), R("ti"), -2.0)
+    lin(R("tib"), R("ti"), 65536.0)
+    ts(R("tm3"), R("dm"), 0.0, ALU.is_equal, col(cE15), ALU.mult)
+    lin(R("q2"), R("i1"), 3.0)
+    tt(R("q2"), R("q2"), R("tm3"), ALU.subtract)
+    tt(R("q1"), R("q2"), R("tm2"), ALU.add)
+    lin(R("i2"), R("i1"), 2.0)
+    lin(R("r15"), R("bo"), col(cE15))
+    lin(R("bo32"), R("bo"), 1.0)
 
-    XT, FT, BT = R("xw", X0, XZ), R("xw", F0, F0 + W), R("bw", 16, 16 + C)
+    XT, FT, BT, E = R("xw", X0, XE), R("xw", F0, F0 + W), R("bw", 16, 16 + C), R("p3", 0, KS)
+    XF, NGE, M, P4 = R("xw", X0, XE + 16), R("gl", 2 * K, 3 * K), R("sz", 0, KS, 17), R("p4", K, 2 * K)
     for v in range(NV):
         last = v == NV - 1
-        z0 = XZ + v * K
-        Z = R("xw", z0, z0 + K)
-        base[0] = v * OPT["period"]
         names.clear()
-        names["last"] = last
-        ub2, ofb, zr = "ub2" + "ab"[v % 2], "ofb" + "ab"[v % 2], "zr" + "ab"[v % 2]
-        mm([(R("p4", 0, 396), full("i1"), R("c255", 0, 396)), (R("p4", 0, K), full("bouc"), Z), (R("p4", K, 2 * K), full("bohc"), Z)]
-           + wrap(R("p4", 384, 396), "wdhc", "xw", z0, z0 + K))
-        cp(R("ub1", 0, 396), R("p4", 0, 396))
-        ts(R(ub2, 0, 396), R("ub1", 0, 396), 1023, ALU.bitwise_and)
-        ts(full("bu"), R(ub2, 384, 396), 0.5, ALU.mult)
-        cp(full("bb"), IND(BT, full("bu")))
+        names["visit"] = v
+        z0 = v * K
+        Z = R("zb", z0, z0 + K)
+        zr = "zr" + "ab"[v % 2]
+        mm([(R("p5", 0, 24), R("i1"), R("c255"))] + wrap(R("p5", 0, 12), "wdhc", every16("zb", z0, z0 + K))
+           + wrap(R("p5", 12, 24), "wduc", every16("zb", z0, z0 + K)))
+        cp(R("uw"), R("p5", 0, 24))
+        ts(R("ua"), R("uw"), 1023, ALU.bitwise_and)
+        ts(R("bu"), R("ua", 0, 12), 0.5, ALU.mult)
+        ts(R("bb"), IND(BT, R("bu")), -63.75, ALU.add)
+        cp(R("kx", 12, 36), R("ua"))
+        mm([(P4, R("i1"), R("c32"))] + unwrap("p4", K, R("kx", 24, 36)))
+        ts(R("d1x", K, 2 * K, 16), R("ua", 0, 12), 0.5, ALU.mult, 16.0, ALU.add)
+        act(R("z2"), Z, bias=2049.5, scale=2.0)
         for k in range(16):
-            if k < GZ:
-                gp("aff", (R(zr, k, 16 * K, 16), Z, [[0, K]], ALU.is_ge, 0.0, 0, 0), R(zr, k, 16 * K, 16), [Z])
+            if k < OPT["gz"]:
+                aff(R(zr, k, 16 * K, 16), Z, [[0, K]], ALU.is_ge, 0.0, 0, 0)
             else:
                 cp(R(zr, k, 16 * K, 16), Z)
-        for src, off, o0, bank, dst in (("fg", "bb", 0, "p1", "gp"), ("fl", "lu", v * K, "p0", "lp")):
-            for j0, j1 in CH:
-                act(R(src, 16 * j0, 16 * j1), IND(FT, R(off, o0 + j0, o0 + j1)), ACT.Identity)
-                mm(wrap(R(bank, j0, j1), "wd", src, 16 * j0, 16 * j1))
-                ts(R(dst, j0, j1), R(bank, j0, j1), float(W), ALU.add)
-        ts(full("kbf"), R(ub2, 384, 396), 0.5, ALU.mult)
-        tt(full("eqb"), IND(R(ub2, 384, 396), R("eo", 0, 12)), R(ub2, K, 2 * K), ALU.is_equal)
-        contest(R("p5", 0, 12), "eqb", full("kbf"))
-        ts(R(ofb, 0, 24, 2), R("p5", 0, 12), 16.0, ALU.add, col(cA), ALU.max)
-        act(full("lf"), R("p0", 0, K), ACT.Identity)
-        act(R("p0", K, 2 * K), full("lf"), ACT.Identity, bias=float(W))
-        for (j0, j1), on in zip(CH, OPT["cl"]):
-            mm(dist(R("p2", j0, j1), "dl", j0, j1, on, "lp", zr))
-        tt(full("egl"), R("p1", 0, K), full("lf"), ALU.is_equal)
-        tt(full("t1"), R("p0", K, 2 * K), R(ub2, 0, K), ALU.mult)
-        act(R("p1", K, 2 * K), full("t1"), ACT.Identity, bias=col(cCK), scale=1.0 / 32)
-        tt(full("mx"), R("p1", 0, K), full("lf"), ALU.max)
-        tt(full("mn"), R("p1", 0, K), full("lf"), ALU.min)
-        mm([(R("p3", 0, K), full("tm0"), R("c255", 0, K))], stop=False)
-        for (j0, j1), on in zip(CH, OPT["cg"]):
-            mm(dist(R("p3", j0, j1), "dg", j0, j1, on, "gp", zr), start=False, stop=False)
-        mm([(R("p3", 0, K), full("ib"), full("egl"))], start=False)
-        act(full("sg"), R("p3", 0, K), ACT.Sign, bias=col(cT5), scale=-1.0)
-        mm([(R("p7", 0, K), full("q2"), full("sg"))])
-        act(full("ohm"), R("p7", 0, K), ACT.Relu, bias=col(cQ2))
-        mm([(R("p4", 0, K), full("bo"), full("ohm"))])
-        mm(wrap(R("p3", 0, 12), "wdb", "ohm", 0, K) + [(R("p3", 0, 12), full("i32"), full("zsv"))])
-        act(full("ex"), R("p4", 0, K), ACT.Identity)
-        cp(full("ofz"), R("p3", 0, 12))
-        tt(full("sz"), IND(full("dg"), full("ofz")), full("ex"), ALU.mult)
-        mm([(R("p3", 0, K), full("i2"), Z), (R("p3", 0, K), full("i1"), full("sz"))])
-        act(full("sz2"), R("p3", 0, K), ACT.Identity, bias=MAG, scale=HALF)
-        act(R("zo", v * K, v * K + K), full("sz2"), ACT.Identity, bias=-MAG)
-        if last:
-            dma("Y", "yz", ("h", "yz"), R("zo", v * K, v * K + K))
-        else:
-            add("G", "send", ("Z", v), [], [R("zo", v * K, v * K + K)])
-            add("N", "arrive", "aZ%d" % (v + 1), [R("xw", z0 + K, z0 + 2 * K)], [])
-        act(full("sf"), R("p2", 0, K), ACT.Sign, bias=col(cNT5) if v == 0 else R("nthr", 0, 1))
-        mm([(R("p6", 0, K), full("ti"), full("sf"))])
-        mm([(R("p6", K, 2 * K), full("q1"), full("sf"))])
-        act(full("nge"), R("p6", 0, K), ACT.Sign, bias=col(cGE), scale=-1.0)
-        act(R("p2", K, 2 * K), R("p6", K, 2 * K), ACT.Relu, bias=col(cQ1))
-        tt(full("t3"), R("p1", K, 2 * K), full("nge"), ALU.mult)
-        tt(full("t4"), R("p0", K, 2 * K), full("t3"), ALU.subtract)
-        ts(full("new"), full("t4"), W - 1, ALU.bitwise_and)
-        tt(R("pgl", 0, K), R("p2", K, 2 * K), full("new"), ALU.mult)
-        if last:
-            cp(full("ylf"), full("new"))
-            dma("Y", "yl", ("h", "yl"), full("ylf"))
-        else:
-            cp(R("ls", v * K, v * K + K), full("new"))
-            add("G", "send", ("L", v), [], [R("ls", v * K, v * K + K)])
-            add("N", "arrive", "aL%d" % (v + 1), [R("lu", (v + 1) * K, (v + 2) * K)], [])
-        scatter(full("bw"), ofb, "new", 0)
-        if last:
-            cp(full("ybf"), BT)
-            dma("Y", "yb", ("h", "yb"), full("ybf"))
-        D15 = R("dl", 15, 16 * K, 16)
-        mm([(R("p5", 128, 128 + K), full("r15"), full("nge"))])
-        tt(full("sv"), R("p5", 128, 128 + K), D15, ALU.mult)
-        mm([(R("p0", 0, K), full("i2"), Z), (R("p0", 0, K), full("i1"), D15), (R("p0", 0, K), full("i1"), full("sv"))])
-        act(full("sv2"), R("p0", 0, K), ACT.Identity, bias=MAG, scale=HALF)
-        act(DAT(1), full("sv2"), ACT.Identity, bias=-MAG)
-        mm([(R("p6", 0, K), full("i2"), full("nge")), (R("p6", 0, K), full("q2"), full("sg"))])
-        act(R("p6", 0, K), R("p6", 0, K), ACT.Relu, bias=col(cQ2), acc=None if last else R("acc", 0, 1))
-        tt(R("pgl", K, 2 * K), R("p6", 0, K), full("mx"), ALU.mult)
-        tt(R("pgl", 2 * K, 3 * K), R("p6", 0, K), full("mn"), ALU.mult)
-        mm([(R("p7", 0, 2 * K), full("bo"), R("pgl", 0, 2 * K))])
-        mm(wrap(R("p4", 400, 424), "wd", "pgl", 0, 2 * K))
-        act(full("hir"), R("p7", 0, 2 * K), ACT.Identity)
-        act(full("hiw"), R("p4", 400, 424), ACT.Identity)
-        mm([(R("p1", K, 2 * K), full("bo"), R("pgl", 2 * K, 3 * K))])
-        tt(full("eqh"), IND(full("hiw"), full("eo")), full("hir"), ALU.is_equal)
-        contest(R("p2", 0, 24), "eqh", full("hiw"))
-        if last:
-            ts(R("ofw", 0, 24, 2), R("p2", 0, 12), 16.0, ALU.add, col(cA), ALU.max)
-        else:
-            ts(R("off", 1, 24, 2), R("p2", 0, 12), float(X0), ALU.add, col(cAX), ALU.max)
-        act(full("lo2"), R("p1", K, 2 * K), ACT.Identity, bias=col(cCR), scale=1.0 / 16)
-        act(full("lo3"), full("lo2"), ACT.Identity, bias=MAG)
-        act(DAT(0), full("lo3"), ACT.Identity, bias=-MAG)
-        if last:
-            for jj in range(11, -1, -1):
-                cp(IND(R("xw", X0 - 16, XZ), R("ofw", 2 * jj, 2 * jj + 1)), DJ(jj, 1, 2))
-        ts(R("off", 0, 24, 2), R("p2", 12, 24), float(F0 + W), ALU.add, col(cA), ALU.max)
-        for jj in range(11, -1, -1):
-            if last:
-                cp(IND(R("xw", 0, X0 - 16), R("off", 2 * jj, 2 * jj + 1)), DJ(jj, 0, 1))
+        for j0, j1 in PIECES:
+            jm = j0 + (OPT["fv"] if j1 == K else 0)
+            if jm > j0:
+                cp(R("fl", 16 * j0, 16 * jm), IND(FT, R("lu", z0 + j0, z0 + jm)))
+            act(R("fl", 16 * jm, 16 * j1), IND(FT, R("lu", z0 + jm, z0 + j1)))
+            mm(wrap(R("p0", j0, j1), "wd", every16("fl", 16 * j0, 16 * j1)))
+            ts(R("lp", j0, j1), R("p0", j0, j1), 1024.0, ALU.add)
+        act(R("lf"), R("p0", 0, K), bias=1024.0)
+        act(R("lg"), R("p0", 0, K), bias=-1024.0)
+        for j0, j1 in PIECES:
+            act(R("fg", 16 * j0, 16 * j1), IND(FT, R("bb", j0, j1)))
+            mm([(R("p1", j0, j1), R("i1"), R("c1k", j0, j1))] + wrap(R("p1", j0, j1), "wd", every16("fg", 16 * j0, 16 * j1)))
+            tt(R("egl", j0, j1), R("p1", j0, j1), R("lg", j0, j1), ALU.not_equal)
+            tt(R("gq", j0, j1), R("p1", j0, j1), R("egl", j0, j1), ALU.mult)
+            ts(R("gp", j0, j1), R("gq", j0, j1), float(W), ALU.add)
+        tt(R("t1"), P4, R("lf"), ALU.mult)
+        act(R("rp"), R("t1"), bias=col(cCK), scale=1.0 / 32)
+        for (j0, j1), on in zip(PIECES, OPT["al"]):
+            lo, hi, out = 16 * j0, 16 * j1, R("p2", j0, j1)
+            tt(R("dl", lo, hi), IND(XF, R("lp", j0, j1)), R(zr, lo, hi), ALU.subtract)
+            if on == "S":
+                act(R("rdl", lo, hi), R("dl", lo, hi), ACT.Abs)
+                mm(wrap(out, "wdh", every16("rdl", lo, hi)))
             else:
-                cp(IND(R("xw", 0, XZ), R("off", 2 * jj, 2 * jj + 2)), DJ(jj, 0, 2))
+                ts(R("rdl", lo, hi), R("dl", lo, hi), 0.0, ALU.max)
+                mm(wrap(out, "wdn", every16("dl", lo, hi)) + wrap(out, "wd2", every16("rdl", lo, hi)))
+        mm([(E, R("boh"), R(x)) for x in ("tth", "ttl")], stop=False)
+        for j0, j1 in PIECES:
+            lo, hi, q = 16 * j0, 16 * j1, S(j0 // 16, j1 // 16)
+            tt(R("dg", lo, hi), IND(XF, R("gp", j0, j1)), R(zr, lo, hi), ALU.subtract)
+            act(R("rdg", q, ALL, S(0, 16)), R("dg", lo, hi), ACT.Abs)
+            mm(wrap(R("p3", 17 * q.start, 17 * q.stop), "wdh", lambda a: R("rdg", q, a, ALL)), start=False, stop=j0 == 0, group=[E])
+        scan(back("sz"), back("p3"), back("pz"))
+        act(R("sf"), R("p2", 0, K), ACT.Sign, bias=col(cNT5) if v == 0 else R("nthr", 0, 1), scale=1 / H)
+        mm([(R("p6", 0, K), R("ti"), R("sf"))])
+        mm([(R("p6", K, 2 * K), R("q1"), R("sf"))])
+        act(NGE, R("p6", 0, K), ACT.Sign, bias=col(cGE), scale=-1.0)
+        act(R("p2", K, 2 * K), R("p6", K, 2 * K), ACT.Relu, bias=col(cQ1))
+        mm([(P4, a, b) for a, b in ((R("i32"), R("lf")), (R("tib"), R("ones", 0, K)), (R("tib"), R("sf")))])
+        tt(R("t4"), P4, R("rp"), ALU.min)
+        ts(R("new"), R("t4"), W - 1, ALU.bitwise_and)
+        if last:
+            cp(R("ylf"), R("new"))
+            dma("Y", "yl", ("h", "yl"), R("ylf"))
+        else:
+            cp(R("ls", z0, z0 + K), R("new"))
+            add("G", "send", ("L", v), [], [R("ls", z0, z0 + K)])
+            add("N", "arrive", "aL%d" % (v + 1), [R("lu", z0 + K, z0 + 2 * K)], [])
+        tt(R("pgl"), R("p2", K, 2 * K), R("new"), ALU.mult)
+        mm(wrap(R("p5", 48, 60), "wd", every16("pgl", 0, K)))
+        cp(R("kx", 0, 12), R("p5", 48, 60))
+        act(R("d1x", 0, K, 16), R("p5", 48, 60), bias=float(X0))
+        mm([(R("p7", 0, 2 * K), R("i1"), R("cbig"))] + contest("p7", 2 * K, R("kx", 0, 24)))
+        act(R("dx"), R("p7", 0, 2 * K), ACT.Abs, scale=8192.0)
+        scan(R("sx"), R("dx"), R("d1x"))
+        cp(R("ofb", 0, 24, 2), R("sx", K + 15, 2 * K, 16))
+        ts(R("ofw", 0, 24, 2), R("sx", 15, K, 16), 16.0 - X0, ALU.add)
+        ts(R("nb"), R("new"), 64.0, ALU.add)
+        for jj in range(11, -1, -1):
+            act(IND(R("bw"), R("ofb", 2 * jj, 2 * jj + 1)), R("nb", 16 * jj, 16 * jj + 16), ACT.Silu)
+        if last:
+            ts(R("ybf"), BT, MAG - 64, ALU.add, MAG, ALU.subtract)
+            dma("Y", "yb", ("h", "yb"), R("ybf"))
+        D15 = R("dl", 15, 16 * K, 16)
+        mm([(R("p5", 128, 128 + K), R("r15"), NGE)])
+        tt(R("sv"), R("p5", 128, 128 + K), D15, ALU.mult)
+        mm([(R("p4", 0, K), R("i2"), Z), (R("p4", 0, K), R("i1"), D15), (R("p4", 0, K), R("i1"), R("sv"))])
+        act(R("sv2"), R("p4", 0, K), bias=MAG, scale=HALF)
+        act(DAT(1), R("sv2"), bias=-MAG)
+        for jj in range(11, -1, -1):
+            cp(IND(R("xw", X0 - 16, XE), R("ofw", 2 * jj, 2 * jj + 1)), DAT(1, jj))
+        if last:
+            dma("Y", "yx", ("h", "yx"), XT)
+        cp(R("ofz"), M)
+        tt(R("zs"), IND(R("dg"), R("ofz")), R("z2"), ALU.add)
+        ts(R("zo", z0, z0 + K), R("zs"), 0.5, ALU.mult, -1025.0, ALU.add)
+        if last:
+            dma("Y", "yz", ("h", "yz"), R("zo", z0, z0 + K))
+        else:
+            add("G", "send", ("Z", v), [], [R("zo", z0, z0 + K)])
+            add("N", "arrive", "aZ%d" % (v + 1), [R("zb", z0 + K, z0 + 2 * K)], [])
+        act(R("gl", 0, K), IND(R("fg"), R("ofz")))
+        cp(R("gl", K, 2 * K), IND(R("fl"), R("ofz")))
+        mm([(R("p1", 0, 36), R("i1"), R("c1025"))] + wrap(R("p1", 0, 36), "wd", every16("gl", 0, 3 * K)))
+        tt(R("mg"), M, R("p1", 24, 36), ALU.is_lt)
+        cp(R("lm"), R("p1", 12, 24))
+        tt(R("hi0"), R("p1", 0, 12), R("lm"), ALU.max)
+        tt(R("lo16"), R("p1", 0, 12), R("lm"), ALU.min)
+        tt(R("kf"), R("hi0"), R("mg"), ALU.mult)
+        ts(R("d1f", 0, K, 16), R("kf"), F0 - 1.0, ALU.add)
+        mm([(R("p6", 0, K), R("i1"), R("cbig", 0, K))], stop=False, after=[R("p2", K, 2 * K)])
+        mm(contest("p6", K, R("kf")), start=False)
+        mm(unwrap("p4", K, R("lo16")), each=True)
+        act(R("df"), R("p6", 0, K), ACT.Abs, scale=8192.0)
+        scan(R("sq"), R("df"), R("d1f"))
+        cp(R("off", 0, 24, 2), R("sq", 15, K, 16))
+        act(DAT(0), P4, bias=col(cF1), scale=1.0 / 16)
+        for jj in range(11, -1, -1):
+            cp(IND(R("xw", 0, X0 - 16), R("off", 2 * jj, 2 * jj + 1)), DAT(0, jj))
         if not last:
-            mm([(R("p5", 64, 65), full("bo32"), R("acc", 0, 1))])
-            act(R("acc", 1, 2), R("p5", 64, 65), ACT.Identity, bias=-7.5 / 16, scale=1.0 / 16)
-            act(R("acc", 2, 3), R("acc", 1, 2), ACT.Identity, bias=MAG)
-            act(R("acc", 3, 4), R("acc", 2, 3), ACT.Identity, bias=-16 * MAG, scale=16.0)
-            act(R("nthr", 1, 2), R("p5", 64, 65), ACT.Identity, bias=col(cNT5), scale=-1.0)
-            act(R("nthr", 0, 1), R("nthr", 1, 2), ACT.Identity, bias=R("acc", 3, 4))
-    dma("Y", "yx", ("h", "yx"), XT)
-    mm([(R("p0", 0, 512, p=P32), R("wy", 3 - s, 35 - s), R("xw", F0 + 512 * s, F0 + 512 + 512 * s)) for s in range(4)])
-    act(R("yff", 0, 512, p=P32), R("p0", 0, 512, p=P32), ACT.Identity, bias=float(W))
-    dma("S", "yf", ("h", "yf"), R("yff", 0, 512, p=P32))
+            act(R("junk"), R("mg"), acc=R("acc", 0, 1))
+            mm([(R("p5", 64, 65), R("bo32"), R("acc", 0, 1))])
+            act(R("a16", 0, 1), R("p5", 64, 65), bias=130 - 7.5 / 16, scale=1.0 / 16)
+            act(R("nthr", 1, 2), R("p5", 64, 65), bias=col(cNT6), scale=-1.0)
+            act(R("nthr", 0, 1), R("a16", 0, 1), bias=R("nthr", 1, 2), scale=16.0)
+    mm(wrap(R("p2", 0, 128), "wd", lambda s: R("xw", F0 + 128 * s, F0 + 128 + 128 * s)))
+    act(R("yff"), R("p2", 0, 128), bias=1024.0)
+    dma("S", "yf", ("h", "yf"), R("yff"))
     return ops
-
-
-def meet(a, b):
-    if a[4] > 1 and a[4] == b[4] and (a[2] - b[2]) % a[4]:
-        return False
-    return a[1] == b[1] and a[2] < b[3] and b[2] < a[3]
 
 
 def depend(ops):
@@ -368,32 +400,43 @@ def depend(ops):
         else:
             for x, isw in [(x, False) for x in o["r"]] + [(x, True) for x in o["w"]]:
                 for j, y, yw in seen.get(x[1], []):
-                    if meet(x, y) and (isw or yw):
-                        (soft if o["eng"] == "P" and ops[j]["eng"] == "P" else hard).add(j)
-        plain = [x for x in o["w"] if x[6] is None]
-        for x in set(plain):
-            if x[4] == 1 and x[5] is None and o["kind"] != "mm":
-                seen[x[1]] = [e for e in seen.get(x[1], []) if not (x[2] <= e[1][2] and e[1][3] <= x[3])]
+                    if y & x[4] and (isw or yw):
+                        (soft if o["eng"] == ops[j]["eng"] == "P" else hard).add(j)
+        if o["kind"] != "mm":
+            for x in o["w"]:
+                if x[3] is None:
+                    seen[x[1]] = [e for e in seen.get(x[1], []) if e[1] & ~x[4]]
         for lst, isw in ((o["r"], False), (o["w"], True)):
-            for x in set(y[:5] for y in lst):
-                seen.setdefault(x[1], []).append((i, x, isw))
+            both = {}
+            for x in lst:
+                both[x[1]] = both.get(x[1], 0) | x[4]
+            for n, bits in both.items():
+                seen.setdefault(n, []).append((i, bits, isw))
         o["data"], o["soft"] = hard, soft - hard
-        o["banks"] = sorted(set(x[1] for x in o["r"] + o["w"] if psum(x)))
+        o["banks"] = sorted(set(x[1] for x in o["r"] + o["w"] if SCRATCH[x[1]][0] == "psum"))
     return ops
 
 
-def fixed(ops, when):
-    t = []
-    for o in ops:
-        t.append(max([o["base"] + when[o["key"]]] + [t[j] + 0.001 for j in o["data"] | o["soft"]]))
-    order = sorted(range(len(ops)), key=lambda i: (t[i], i))
-    bank = {}
-    for i in order:
+def arrange(ops):
+    key = [(o["visit"] or 0) + WHEN[("i" if o["visit"] is None else "") + o["nth"]] for o in ops]
+    left, after = [len(o["data"] | o["soft"]) for o in ops], [[] for _ in ops]
+    for i, o in enumerate(ops):
+        for j in o["data"] | o["soft"]:
+            after[j].append(i)
+    ready, order, bank = [(key[i], i) for i in range(len(ops)) if not left[i]], [], {}
+    while ready:
+        ready.sort(reverse=True)
+        i = ready.pop()[1]
+        order.append(i)
         o = ops[i]
         o["hard"] = set(o["data"])
         for b in o["banks"]:
             o["hard"] |= set(j for e, j in bank.setdefault(b, {}).items() if e != o["eng"])
             bank[b][o["eng"]] = i
+        for k in after[i]:
+            left[k] -= 1
+            if not left[k]:
+                ready.append((key[k], k))
     return order
 
 
@@ -406,7 +449,7 @@ def rank_program(g, core, T, topo):
         return
     if not PLAN:
         PLAN.append(depend(build()))
-        PLAN.append(fixed(PLAN[0], WHEN))
+        PLAN.append(arrange(PLAN[0]))
     ops, order = PLAN
     Q = {"V": g.vector, "S": g.scalar, "P": g.tensor, "G": g, "Y": g.sync}
 
@@ -417,25 +460,31 @@ def rank_program(g, core, T, topo):
             return T[x[1]][:]
         if x[0] == "i":
             return ap(x[1]).indirect(ap(x[2]))
-        if x[6] is not None:
-            return T[x[1]][x[6][0]]
-        ps = slice(None) if x[5] is None else slice(x[5][0], x[5][1])
-        return T[x[1]][ps, slice(x[2], x[3], x[4]) if x[4] != 1 else slice(x[2], x[3])]
+        return T[x[1]][(ALL if x[3] is None else slice(x[3][0], x[3][1]),) + x[2]]
 
     def route(v):
         s = 1 + v % (N - 1)
         return T.cores[(rank + s) % N], T.cores[(rank - s) % N]
 
-    needed, pos, got = set(), {i: p for p, i in enumerate(order)}, {}
+    pos, known, clock, waits = {i: p for p, i in enumerate(order)}, {e: {} for e in Q}, {}, {}
     for i in order:
-        for e in "VSPG":
-            js = [j for j in ops[i]["hard"] if ops[j]["eng"] == e and ops[j]["kind"] != "dma"]
-            if js:
-                j = max(js, key=pos.get)
-                if pos[j] > got.get((ops[i]["eng"], e), -1):
-                    got[(ops[i]["eng"], e)] = pos[j]
-                    needed.add(j)
-    token, count, waited = {}, {e: 0 for e in "VSPG"}, {}
+        o = ops[i]
+        e = o["eng"]
+        line = i if o["kind"] in ("dma", "arrive") else e
+        if o["kind"] == "arrive":
+            clock[i] = {line: pos[i]}
+            continue
+        waits[i] = []
+        for j in sorted(o["hard"], key=lambda j: -pos[j]):
+            lj = j if ops[j]["kind"] in ("dma", "arrive") else ops[j]["eng"]
+            if ops[j]["kind"] != "send" and known[e].get(lj, -1) < pos[j]:
+                waits[i].append(j)
+                for key, p in clock[j].items():
+                    known[e][key] = max(known[e].get(key, -1), p)
+        clock[i] = dict(known[e])
+        clock[i][line] = pos[i]
+    needed = set(j for w in waits.values() for j in w)
+    token, count = {}, {e: 0 for e in "VSPG"}
     sent = 0
     for i in order:
         o = ops[i]
@@ -443,16 +492,9 @@ def rank_program(g, core, T, topo):
         if kind == "arrive":
             token[i] = (a, len(topo.engines(route(int(a[2:]) - 1)[1], core)))
             continue
-        want = {}
-        for j in o["hard"]:
-            if j in token:
-                s, c = token[j]
-                want[s] = max(want.get(s, 0), c)
         q = Q[e]
-        for s in sorted(want):
-            if waited.get((e, s), 0) < want[s]:
-                q.wait_ge(T.sem[s], want[s])
-                waited[(e, s)] = want[s]
+        for j in waits[i]:
+            q.wait_ge(T.sem[token[j][0]], token[j][1])
         if kind == "dma":
             q.dma_start(ap(a[1]), ap(a[2])).then_inc(T.sem["d_" + a[0]], 16)
             token[i] = ("d_" + a[0], 16)
@@ -464,7 +506,7 @@ def rank_program(g, core, T, topo):
             if a[0] == "L":
                 src, out = T.ls[:, v * K:v * K + K], T.lu[:, (v + 1) * K:(v + 2) * K]
             else:
-                src, out = T.zo[:, v * K:v * K + K], T.xw[:, XZ + (v + 1) * K:XZ + (v + 2) * K]
+                src, out = T.zo[:, v * K:v * K + K], T.zb[:, (v + 1) * K:(v + 2) * K]
             g.remote_dma(out, src, T.sem["a%s%d" % (a[0], v + 1)], T.sem.sent, pid, rid, topo.mask(core, dst))
             sent += len(topo.engines(core, dst))
             continue
@@ -477,16 +519,18 @@ def rank_program(g, core, T, topo):
                 ins = q.tensor_scalar(ap(a[0]), ap(a[1]), ap(a[2]), None, a[4])
             else:
                 ins = q.tensor_scalar(ap(a[0]), ap(a[1]), ap(a[2]), ap(a[3]), a[4], a[5])
+        elif kind == "scan":
+            ins = q.tensor_tensor_scan(ap(a[0]), ap(a[1]), ap(a[2]), 0.0, ALU.min, ALU.max)
         elif kind == "ms":
             ins = q.memset(ap(a[0]), a[1])
+        elif kind == "act" and a[0][0] == "i":
+            ins = q.activation(ap(a[0]), ap(a[1]), a[2])
         elif kind == "act":
             ins = q.activation(ap(a[0]), ap(a[1]), a[2], bias=ap(a[3]), scale=ap(a[4]), accum_out=ap(a[5]))
         elif kind == "mm":
-            begun = []
+            start, stop, each = o["group"]
             for m, (out, l, r) in enumerate(a):
-                first = o["group"][0] and not any(meet(out, y) for y in begun)
-                begun.append(out)
-                ins = q.matmul(ap(out), ap(l), ap(r), first, o["group"][1] and m == len(a) - 1)
+                ins = q.matmul(ap(out), ap(l), ap(r), each or (start and m == 0), each or (stop and m == len(a) - 1))
         elif kind == "iota":
             if SCRATCH[a[0][1]][2] == "int32":
                 ins = q.iota(ap(a[0]), a[1], a[2], a[3])

import numpy as np
from concourse.mybir import AluOpType as ALU, ActivationFunctionType as ACT

W, C, K, NV, N = 2048, 512, 192, 6, 4
MAG = 12582912.0
HALF = 0.5 - 1.0 / 2048
H = 2.0 ** 21
KS = 12 * 17
F0, X0 = 32, 48 + W
XE = X0 + W
PIECES = ((128, K), (64, 128), (0, 64))
OPT = {"gz": 7,
       "fv": 32,
       "al": "SVS"}

ORDER = """iGdsel Vbb Sfl.2 Vdl Sfg iStib Pp0.1 Pp4 Vlp.1 Vdl.1 Vrdl Slg iSwdn iSi32 Slf Pp0.2 Sfg.2 Pp1 Vegl iVc1025 Vlp.2 Vgq
Pp2.1 Vt1 Vgp Vdl.2 Sfg.1 Pp1.2 Vdg Srdl Pp1.1 Srdl.1 Srdg Pp2 Vegl.1 iVcbig Vegl.2 Vgq.1 Vgq.2 Vgp.1 Vgp.2 Vdg.1 Pp2.2 Ssf
iScol.5 Pp3.1 Vdg.2 iVtm2 Pp6 Pp4.1 Srp Srdg.1 Sgl Srdg.2 Pp3.2 Pp6.1 Pp5.2 iGdm+ iGpi+ iGgm+ iGlvl+ iGpos+ iSzb+ iVc255+
iYfwi+ iSthi+ iVones.1+ iVpi.1+ iVtm1+ iVpi+ iVones+ iSlai+ iVcol+ iVwd+ iYbki+ iYxw+ Vt4 iVq1 iVi1+ iVc255.1+ iVc32+ iVbo+
iVcol.1+ iVcol.2+ iVc1k+ iVrdg+ iVcol.3+ iVtm3+ iVq2+ Sp2 Nlu Pp3.3 Pp5.1 Pp4.2 iSbo32 Sz2 Vnew iVpz Vls iVfl iVfg iVdg
iVcbig.1 Vsv Vsvz Vpgl Vylf Vsz Vofz Vgl Sgl.1 iVcol.4+ iVwd.1+ iVcol.7+ iScol.1+ iSr15+ iGrr+ Pp1.3 Pp7 Vzo Vzs Nzb Gzr.3+
Gzr.5+ Gzr.2+ Gzr.4+ Gzr.6+ Gzr+ Gzr.1+ GL iGsel+ GZ Vkx.1 Vkxz.1 Yyl Yyz Yyx Yyb Sd1x iSd1x iSd1f Ssv2 Vnb Vnbz Vlm Vlo16 Vkf
Vmg Vhi0 Vd1x iVcol.8 Vd1f iVfwh+ Ssv2z Sdatz Sdx Sdxz Vsx Vsxz Vofb Vofbz Pp6.2 Pp6.3 Pp4.3 Sdf Sdfz Vsq Vsqz Vofw Vofwz Voff
Voffz Sdat Vxw Vxwz Sjunk Vxwz.1 Sdat.1 Sdatz.1 Sbwz Sbwz.1 Sbwz.2 Sbwz.3 Sbwz.4 Sbwz.5 Sbwz.6 Sbwz.7 Sbwz.8 Sbwz.9 Sbwz.10
Sbwz.11 Vxwz.2 Vxwz.3 Vxwz.4 Vxwz.12 Vxwz.5 Vxwz.13 Vxwz.6 Sbw Vxwz.14 Vxwz.7 Pp5.3 Vxwz.15 Snthr Vxwz.8 Sbw.1 Vxwz.16 Sa16
Vxwz.9 Vxwz.17 Sbw.2 Vxwz.10 Sbw.6 Vxwz.18 Sbw.7 Vxwz.11 Vxwz.19 Sbw.8 Vybf Sbw.9 Vxwz.20 Sbw.3 Vxwz.21 Snthr.1 Vxwz.22 iVthi+
Vxwz.23 iScol.4+ iVcol.6+ iVlu+ iVq2.1+ Vxw.12 iVwduc+ Vzr.1+ Pp2.3 Syff Syf Vxw.13 iVcol.9+ iVcol.5+ iPp2+ iPp7+ Pp5+ Pp3+
iPp6+ iPp4+ Sbw.10 Vxw.1 Vxw.14 Vzr.4+ Vxw.15 Vxw.2 Vxw.16 Vxw.3 Vxw.17 iScol.6+ iSpz+ iSboh+ iSwdh+ iScol+ iScol.2+
iSwd2+ iSxw.1+ iScol.3+ iSi2+ iSxw+ Vxw.4 Vxw.18 Sbw.4 Vxw.5 Vxw.19 Vxw.6 Vxw.20 Vxw.7 Vxw.21 iVwdhc+ iVxw+ Vzr.7+ iVxw.1+
iVcol.10+ iVxw.2+ Vxw.22 Vxw.8 Vxw.23 iVbw+ Vxw.9 iVttl+ Vuw+ Sbw.5 Sbw.11 Sfl+ iSd1x.1+ Sfl.1+ Vfl+ Vua+ Pp0+ Vzr.2+ Vbu+
Vkx+ Vkxz+ Vxw.10 Vzr.5+ Vxw.11 Vzr+ iVttl.1+ iVc1025.1+ Vzr.3+ Vzr.6+ Vlp+ Vzr.8+ iVtth+ iVti+""".split()
WHEN = {x.strip("+-") + ("" if "." in x else ".0"): i / len(ORDER) - x.count("+") + x.count("-") for i, x in enumerate(ORDER)}
OWN_END = "Vxw Sbw Vsx Vofb Vofw Vnb Sdx Ssv2 Sdat Vsv Vkx Vsq Voff Sdf".split()
ON_SCALAR = "wdh wdn wd2 boh i32 tib pz i2 r15 d1x d1f bo32".split()

SCRATCH = {
    "xw": ("sbuf", [128, XE + 16], "bfloat16"),
    "bw": ("sbuf", [128, 16 + C], "float32"),
    "dat": ("sbuf", [128, 12, 32], "bfloat16"),
    "sel": ("sbuf", [128, 16, 128], "bfloat16"),
    "dsel": ("sbuf", [128, 15, 128], "bfloat16"),
    "rdg": ("sbuf", [128, 12, 16, 17], "bfloat16"),
}
for _x in "pos lvl".split():
    SCRATCH[_x] = ("sbuf", [128, 12, 17], "float32")
for _names, _n, _dt in (
        ("lu ls", NV * K, "uint16"), ("zb zo", NV * K, "bfloat16"), ("ones", W, "bfloat16"),
        ("fl fg dg", 16 * K + 16, "bfloat16"), ("dl rdl zra zrb", 16 * K, "bfloat16"),
        ("uw ua", 24, "int32"), ("ofb ofw off", 24, "uint16"), ("lai t4 new", K, "int32"),
        ("thi pi", 4, "int32"), ("fwi bki", 512, "int32"), ("fwh", 512, "float16"),
        ("col", 24, "float32"), ("gm dm bo32 i32", 128, "float32"),
        ("bo boh i1 i2 ti tib q1 q2 r15 tm1 tm2 tm3", 128, "bfloat16"),
        ("wd wdhc wduc wdh wdn wd2", 144, "bfloat16"), ("rr", 512, "bfloat16"),
        ("c255", 24, "bfloat16"), ("c1025", 36, "float16"), ("gl", 3 * K, "bfloat16"), ("bu ofz", 12, "uint16"),
        ("tth ttl", KS, "bfloat16"), ("cbig dx", 2 * K, "bfloat16"), ("d1x sx", 2 * K, "float32"),
        ("kx", 36, "float16"), ("kf lo16", 12, "float16"), ("mg hi0 lm junk", 12, "float32"),
        ("bb lp gp", K, "uint16"), ("c32 c1k egl sf sv df", K, "bfloat16"), ("pgl zs", K, "float16"),
        ("lf lg gq rp nb t1 sv2 z2 ylf d1f sq", K, "float32"), ("a16", 4, "bfloat16"), ("pz sz", KS, "float32"),
        ("acc nthr", 4, "float32"), ("ybf", 512, "float32"), ("yff", 128, "float32")):
    for _x in _names.split():
        SCRATCH[_x] = ("sbuf", [128, _n], _dt)
for _b in range(8):
    SCRATCH["p%d" % _b] = ("psum", [128, 512], "float32")

DMAS = ["fw", "x", "bk", "zz", "la", "th", "yx", "yf", "yb", "yl", "yz"]
SEMAPHORES = (["eV", "eS", "eP", "eG", "sent"] + ["d_" + n for n in DMAS]
              + ["aL%d" % v for v in range(1, NV)] + ["aZ%d" % v for v in range(1, NV)])

cA, cG, cCK, cGE, cQ1, cQ2, cHC, cUC, cF0, cF1, cNT5, cNT6, cE15, cAX, cA16, cTH, cTL = range(17)
ALL = slice(None)


def S(lo, hi, step=1):
    return slice(lo, hi, step)


def R(name, *idx, p=None):
    if idx and all(isinstance(i, int) for i in idx) and len(SCRATCH[name][1]) == 2:
        idx = (slice(*idx),)
    shape = SCRATCH[name][1][1:]
    cols = np.arange(int(np.prod(shape))).reshape(shape)[idx].reshape(-1)
    bits = np.zeros(int(np.prod(shape)), np.uint8)
    bits[cols] = 1
    return ("r", name, idx, p, int.from_bytes(np.packbits(bits).tobytes(), "big"), len(cols))


def IND(win, off):
    return ("i", win, off)


def col(c):
    return R("col", c, c + 1)


def regs(x):
    if not isinstance(x, tuple):
        return []
    return [x[1], x[2]] if x[0] == "i" else [x]


def build():
    ops, names = [], {}

    def add(eng, kind, args, wr, rd):
        w, r = [], []
        for x in wr:
            if x[0] == "i":
                w.append(x[1])
                r.append(x[2])
            else:
                w.append(x)
        for x in rd:
            r.extend(regs(x))
        key = eng + (w[0][1][:2] if w and w[0][1][:2] == "zr" else w[0][1] if w else args[0])
        if names.get("visit") == NV - 1 and key in OWN_END:
            key += "z"
        names[key] = names.get(key, -1) + 1
        ops.append({"eng": eng, "kind": kind, "args": args, "w": w, "r": r, "key": key, "nth": "%s.%d" % (key, names[key]),
                    "visit": names.get("visit")})

    def cp(out, a):
        add("V", "copy", (out, a), [out], [a])

    def tt(out, a, b, op):
        add("V", "tt", (out, a, b, op), [out], [a, b])

    def ts(out, a, s1, o1, s2=None, o2=None):
        add("V", "ts", (out, a, s1, s2, o1, o2), [out], [a, s1, s2])

    def scan(out, a, b):
        add("V", "scan", (out, a, b), [out], [a, b])

    def ms(out, c):
        add("V", "ms", (out, c), [out], [])

    def act(out, a, f=ACT.Identity, bias=0.0, scale=1.0, acc=None):
        add("S", "act", (out, a, f, bias, scale, acc), [out] + ([acc] if acc else []), [a, bias, scale])

    def lin(out, a, m, b=0.0):
        if out[1] in ON_SCALAR:
            act(out, a, bias=b, scale=m)
        else:
            ts(out, a, m, ALU.mult, b, ALU.add)

    def mm(lst, start=True, stop=True, each=False, after=(), group=()):
        add("P", "mm", lst, [x[0] for x in lst] + list(group), [x[1] for x in lst] + [x[2] for x in lst] + list(after))
        ops[-1]["group"] = (start, stop, each)

    def iota(out, pat, base, cm):
        add("G", "iota", (out, pat, base, cm), [out], [])

    def aff(out, a, pat, op, fill, base, cm):
        add("G", "aff", (out, a, pat, op, fill, base, cm), [out], [a])

    def dma(q, name, out, a):
        add(q, "dma", (name, out, a), [out] if out[0] == "r" else [], [a] if a[0] == "r" else [])

    def wrap(out, name, part):
        return [(out, R(name, 15 - a, 143 - a), part(a)) for a in range(16)]

    def every16(name, lo, hi):
        return lambda a: R(name, lo + a, hi, 16)

    def unwrap(bank, lo, a16):
        return [(R(bank, lo + a, lo + K, 16), R("sel", a, ALL), a16) for a in range(16)]

    def contest(bank, n, key):
        return [(R(bank, s, n, 16), R("dsel", s - 1, ALL), key) for s in range(1, 16)]

    def DAT(t, jj=ALL):
        return R("dat", jj, S(16 * t, 16 * t + 16))

    def back(name):
        return R(name, S(KS - 1, None, -1))

    P32 = (0, 32)
    dma("Y", "fw", R("fwi", p=P32), ("h", "fw"))
    dma("S", "zz", R("zb", 0, K), ("h", "zz"))
    dma("S", "la", R("lai"), ("h", "la"))
    dma("Y", "x", R("xw", X0, XE), ("h", "x"))
    dma("S", "th", R("thi", 0, 1), ("h", "th"))
    dma("Y", "bk", R("bki"), ("h", "bk"))
    ts(R("bw", 16, 16 + C), R("bki"), 64.0, ALU.add)
    ms(R("ones", 0, 512), 1.0)
    ms(R("ones", 512, W), 1.0)
    iota(R("pi", 0, 1), [[0, 1]], 0, 1)
    iota(R("gm"), [[1, 8], [0, 16]], 0, 0)
    aff(R("rr", p=P32), R("ones", 0, 512, p=P32), [[-1, 4], [-4, 8], [0, 16]], ALU.is_equal, 0.0, 0, 1)
    iota(R("dm"), [[1, 128]], 0, -1)
    iota(R("pos"), [[0, 12], [1, 17]], 0, 0)
    iota(R("lvl"), [[256, 12], [1, 17]], 0, 0)
    aff(R("sel"), R("ones"), [[-1, 16], [-16, 8], [0, 16]], ALU.is_equal, 0.0, 0, 1)
    aff(R("dsel"), R("sel", S(0, 15), ALL), [[0, 15], [-1, 128]], ALU.not_equal, -1.0, 0, 1)
    ts(R("pi", 1, 2), R("pi", 0, 1), 15, ALU.bitwise_and)
    ts(R("pi", 2, 3), R("pi", 0, 1), 4, ALU.arith_shift_right)
    cp(R("col", cA, cG + 1), R("pi", 1, 3))
    for c, m, b in ((cHC, 28.0, 78.0), (cUC, 10.0, 5.0), (cCK, 613.0, -0.484375), (cGE, -1.0, -1.0), (cQ2, -2.0, 0.0),
                    (cAX, 1.0, X0 - 16.0), (cA16, 16.0, 0.0)):
        act(col(c), col(cA), bias=b, scale=m)
    ts(col(cE15), col(cA), 15.0, ALU.is_equal)
    ts(col(cF1), col(cA), 8.0, ALU.is_lt, -384.0 * 16, ALU.mult)
    ts(col(cF0), col(cF1), col(cA), ALU.add, 1.0 / 16, ALU.mult)
    ts(col(cF1), col(cF0), 128 - 8.5 / 16, ALU.add)
    ts(col(cF0), col(cF0), 128 - 7.5 / 16, ALU.add)
    tt(col(cQ1), col(cQ2), col(cE15), ALU.add)
    ts(R("bo"), R("gm"), col(cG), ALU.is_equal)
    ms(R("wd"), 0.0)
    cp(R("wd", 15, 143, 16), R("bo", 0, 128, 16))
    for name, f in (("wdhc", col(cHC)), ("wduc", col(cUC)), ("wdh", H), ("wdn", -H), ("wd2", 2 * H)):
        lin(R(name), R("wd"), f)
    ts(R("i1"), R("dm"), 0.0, ALU.is_equal)
    ms(R("c255", 0, 12), 510.0)
    ms(R("c255", 12, 24), 255.0)
    cp(R("fwh", p=P32), R("fwi", p=P32))
    for s, bank in enumerate(("p6", "p7", "p2", "p4")):
        mm([(R(bank), R("rr", 128 * s, 128 * s + 128, p=P32), R("fwh", p=P32))])
        if s % 2:
            ts(R("xw", F0 + 512 * s, F0 + 512 + 512 * s), R(bank), 1.0 / 16, ALU.mult, col(cF0), ALU.add)
        else:
            act(R("xw", F0 + 512 * s, F0 + 512 + 512 * s), R(bank), bias=col(cF0), scale=1.0 / 16)
    cp(R("lu", 0, K), R("lai"))
    for name in ("fl", "fg", "dg"):
        ms(R(name, 16 * K, 16 * K + 16), 0.0)
    ms(R("rdg", ALL, ALL, 16), 0.0)
    ms(R("xw", XE, XE + 16), 8192.0)
    ms(R("c1025", 0, 24), 1025.0)
    ms(R("c32"), 32.0)
    ms(R("c1k"), -1024.0)
    ts(col(cNT5), R("thi", 0, 1), -1.0, ALU.mult, -0.5, ALU.add)
    ts(col(cNT6), R("thi", 0, 1), -1.0, ALU.mult, -0.5 - 16 * 130, ALU.add)
    ts(R("thi", 1, 2), R("thi", 0, 1), 4080, ALU.bitwise_and)
    ts(col(cTH), R("thi", 1, 2), -1.0, ALU.mult)
    tt(col(cTL), col(cNT5), col(cTH), ALU.subtract)
    ts(R("tth"), R("pos"), col(cA), ALU.is_equal, col(cTH), ALU.mult)
    ts(R("ttl"), R("pos"), col(cA), ALU.is_equal, col(cTL), ALU.mult)
    ms(R("ttl", 16, KS, 17), -1.0)
    lin(R("boh"), R("bo"), H)
    lin(R("i32"), R("i1"), 1.0)
    lin(R("pz"), R("lvl"), 1.0, col(cA16))
    ms(R("pz", 16, KS, 17), 16.0 * K)
    lin(R("c1025", 24, 36), R("lvl", ALL, 16), 1.0, col(cA16))
    POS = R("pos", ALL, S(0, 16))
    for t, c in enumerate((cAX, cA)):
        ts(R("cbig", K * t, K * t + K), POS, col(cA), ALU.is_gt, 4096.0, ALU.mult)
        lin(R("d1x", K * t, K * t + K), POS, 0.0, col(c))
    lin(R("d1f"), POS, 0.0, col(cA))
    ts(R("tm1"), R("dm"), 0.0, ALU.is_ge)
    tt(R("ti"), R("tm1"), R("bo"), ALU.mult)
    lin(R("tm2"), R("ti"), -2.0)
    lin(R("tib"), R("ti"), 65536.0)
    ts(R("tm3"), R("dm"), 0.0, ALU.is_equal, col(cE15), ALU.mult)
    lin(R("q2"), R("i1"), 3.0)
    tt(R("q2"), R("q2"), R("tm3"), ALU.subtract)
    tt(R("q1"), R("q2"), R("tm2"), ALU.add)
    lin(R("i2"), R("i1"), 2.0)
    lin(R("r15"), R("bo"), col(cE15))
    lin(R("bo32"), R("bo"), 1.0)

    XT, FT, BT, E = R("xw", X0, XE), R("xw", F0, F0 + W), R("bw", 16, 16 + C), R("p3", 0, KS)
    XF, NGE, M, P4 = R("xw", X0, XE + 16), R("gl", 2 * K, 3 * K), R("sz", 0, KS, 17), R("p4", K, 2 * K)
    for v in range(NV):
        last = v == NV - 1
        names.clear()
        names["visit"] = v
        z0 = v * K
        Z = R("zb", z0, z0 + K)
        zr = "zr" + "ab"[v % 2]
        mm([(R("p5", 0, 24), R("i1"), R("c255"))] + wrap(R("p5", 0, 12), "wdhc", every16("zb", z0, z0 + K))
           + wrap(R("p5", 12, 24), "wduc", every16("zb", z0, z0 + K)))
        cp(R("uw"), R("p5", 0, 24))
        ts(R("ua"), R("uw"), 1023, ALU.bitwise_and)
        ts(R("bu"), R("ua", 0, 12), 0.5, ALU.mult)
        ts(R("bb"), IND(BT, R("bu")), -63.75, ALU.add)
        cp(R("kx", 12, 36), R("ua"))
        mm([(P4, R("i1"), R("c32"))] + unwrap("p4", K, R("kx", 24, 36)))
        ts(R("d1x", K, 2 * K, 16), R("ua", 0, 12), 0.5, ALU.mult, 16.0, ALU.add)
        act(R("z2"), Z, bias=2049.5, scale=2.0)
        for k in range(16):
            if k < OPT["gz"]:
                aff(R(zr, k, 16 * K, 16), Z, [[0, K]], ALU.is_ge, 0.0, 0, 0)
            else:
                cp(R(zr, k, 16 * K, 16), Z)
        for j0, j1 in PIECES:
            jm = j0 + (OPT["fv"] if j1 == K else 0)
            if jm > j0:
                cp(R("fl", 16 * j0, 16 * jm), IND(FT, R("lu", z0 + j0, z0 + jm)))
            act(R("fl", 16 * jm, 16 * j1), IND(FT, R("lu", z0 + jm, z0 + j1)))
            mm(wrap(R("p0", j0, j1), "wd", every16("fl", 16 * j0, 16 * j1)))
            ts(R("lp", j0, j1), R("p0", j0, j1), 1024.0, ALU.add)
        act(R("lf"), R("p0", 0, K), bias=1024.0)
        act(R("lg"), R("p0", 0, K), bias=-1024.0)
        for j0, j1 in PIECES:
            act(R("fg", 16 * j0, 16 * j1), IND(FT, R("bb", j0, j1)))
            mm([(R("p1", j0, j1), R("i1"), R("c1k", j0, j1))] + wrap(R("p1", j0, j1), "wd", every16("fg", 16 * j0, 16 * j1)))
            tt(R("egl", j0, j1), R("p1", j0, j1), R("lg", j0, j1), ALU.not_equal)
            tt(R("gq", j0, j1), R("p1", j0, j1), R("egl", j0, j1), ALU.mult)
            ts(R("gp", j0, j1), R("gq", j0, j1), float(W), ALU.add)
        tt(R("t1"), P4, R("lf"), ALU.mult)
        act(R("rp"), R("t1"), bias=col(cCK), scale=1.0 / 32)
        for (j0, j1), on in zip(PIECES, OPT["al"]):
            lo, hi, out = 16 * j0, 16 * j1, R("p2", j0, j1)
            tt(R("dl", lo, hi), IND(XF, R("lp", j0, j1)), R(zr, lo, hi), ALU.subtract)
            if on == "S":
                act(R("rdl", lo, hi), R("dl", lo, hi), ACT.Abs)
                mm(wrap(out, "wdh", every16("rdl", lo, hi)))
            else:
                ts(R("rdl", lo, hi), R("dl", lo, hi), 0.0, ALU.max)
                mm(wrap(out, "wdn", every16("dl", lo, hi)) + wrap(out, "wd2", every16("rdl", lo, hi)))
        mm([(E, R("boh"), R(x)) for x in ("tth", "ttl")], stop=False)
        for j0, j1 in PIECES:
            lo, hi, q = 16 * j0, 16 * j1, S(j0 // 16, j1 // 16)
            tt(R("dg", lo, hi), IND(XF, R("gp", j0, j1)), R(zr, lo, hi), ALU.subtract)
            act(R("rdg", q, ALL, S(0, 16)), R("dg", lo, hi), ACT.Abs)
            mm(wrap(R("p3", 17 * q.start, 17 * q.stop), "wdh", lambda a: R("rdg", q, a, ALL)), start=False, stop=j0 == 0, group=[E])
        scan(back("sz"), back("p3"), back("pz"))
        act(R("sf"), R("p2", 0, K), ACT.Sign, bias=col(cNT5) if v == 0 else R("nthr", 0, 1), scale=1 / H)
        mm([(R("p6", 0, K), R("ti"), R("sf"))])
        mm([(R("p6", K, 2 * K), R("q1"), R("sf"))])
        act(NGE, R("p6", 0, K), ACT.Sign, bias=col(cGE), scale=-1.0)
        act(R("p2", K, 2 * K), R("p6", K, 2 * K), ACT.Relu, bias=col(cQ1))
        mm([(P4, a, b) for a, b in ((R("i32"), R("lf")), (R("tib"), R("ones", 0, K)), (R("tib"), R("sf")))])
        tt(R("t4"), P4, R("rp"), ALU.min)
        ts(R("new"), R("t4"), W - 1, ALU.bitwise_and)
        if last:
            cp(R("ylf"), R("new"))
            dma("Y", "yl", ("h", "yl"), R("ylf"))
        else:
            cp(R("ls", z0, z0 + K), R("new"))
            add("G", "send", ("L", v), [], [R("ls", z0, z0 + K)])
            add("N", "arrive", "aL%d" % (v + 1), [R("lu", z0 + K, z0 + 2 * K)], [])
        tt(R("pgl"), R("p2", K, 2 * K), R("new"), ALU.mult)
        mm(wrap(R("p5", 48, 60), "wd", every16("pgl", 0, K)))
        cp(R("kx", 0, 12), R("p5", 48, 60))
        act(R("d1x", 0, K, 16), R("p5", 48, 60), bias=float(X0))
        mm([(R("p7", 0, 2 * K), R("i1"), R("cbig"))] + contest("p7", 2 * K, R("kx", 0, 24)))
        act(R("dx"), R("p7", 0, 2 * K), ACT.Abs, scale=8192.0)
        scan(R("sx"), R("dx"), R("d1x"))
        cp(R("ofb", 0, 24, 2), R("sx", K + 15, 2 * K, 16))
        ts(R("ofw", 0, 24, 2), R("sx", 15, K, 16), 16.0 - X0, ALU.add)
        ts(R("nb"), R("new"), 64.0, ALU.add)
        for jj in range(11, -1, -1):
            act(IND(R("bw"), R("ofb", 2 * jj, 2 * jj + 1)), R("nb", 16 * jj, 16 * jj + 16), ACT.Silu)
        if last:
            ts(R("ybf"), BT, MAG - 64, ALU.add, MAG, ALU.subtract)
            dma("Y", "yb", ("h", "yb"), R("ybf"))
        D15 = R("dl", 15, 16 * K, 16)
        mm([(R("p5", 128, 128 + K), R("r15"), NGE)])
        tt(R("sv"), R("p5", 128, 128 + K), D15, ALU.mult)
        mm([(R("p4", 0, K), R("i2"), Z), (R("p4", 0, K), R("i1"), D15), (R("p4", 0, K), R("i1"), R("sv"))])
        act(R("sv2"), R("p4", 0, K), bias=MAG, scale=HALF)
        act(DAT(1), R("sv2"), bias=-MAG)
        for jj in range(11, -1, -1):
            cp(IND(R("xw", X0 - 16, XE), R("ofw", 2 * jj, 2 * jj + 1)), DAT(1, jj))
        if last:
            dma("Y", "yx", ("h", "yx"), XT)
        cp(R("ofz"), M)
        tt(R("zs"), IND(R("dg"), R("ofz")), R("z2"), ALU.add)
        ts(R("zo", z0, z0 + K), R("zs"), 0.5, ALU.mult, -1025.0, ALU.add)
        if last:
            dma("Y", "yz", ("h", "yz"), R("zo", z0, z0 + K))
        else:
            add("G", "send", ("Z", v), [], [R("zo", z0, z0 + K)])
            add("N", "arrive", "aZ%d" % (v + 1), [R("zb", z0 + K, z0 + 2 * K)], [])
        act(R("gl", 0, K), IND(R("fg"), R("ofz")))
        cp(R("gl", K, 2 * K), IND(R("fl"), R("ofz")))
        mm([(R("p1", 0, 36), R("i1"), R("c1025"))] + wrap(R("p1", 0, 36), "wd", every16("gl", 0, 3 * K)))
        tt(R("mg"), M, R("p1", 24, 36), ALU.is_lt)
        cp(R("lm"), R("p1", 12, 24))
        tt(R("hi0"), R("p1", 0, 12), R("lm"), ALU.max)
        tt(R("lo16"), R("p1", 0, 12), R("lm"), ALU.min)
        tt(R("kf"), R("hi0"), R("mg"), ALU.mult)
        ts(R("d1f", 0, K, 16), R("kf"), F0 - 1.0, ALU.add)
        mm([(R("p6", 0, K), R("i1"), R("cbig", 0, K))], stop=False, after=[R("p2", K, 2 * K)])
        mm(contest("p6", K, R("kf")), start=False)
        mm(unwrap("p4", K, R("lo16")), each=True)
        act(R("df"), R("p6", 0, K), ACT.Abs, scale=8192.0)
        scan(R("sq"), R("df"), R("d1f"))
        cp(R("off", 0, 24, 2), R("sq", 15, K, 16))
        act(DAT(0), P4, bias=col(cF1), scale=1.0 / 16)
        for jj in range(11, -1, -1):
            cp(IND(R("xw", 0, X0 - 16), R("off", 2 * jj, 2 * jj + 1)), DAT(0, jj))
        if not last:
            act(R("junk"), R("mg"), acc=R("acc", 0, 1))
            mm([(R("p5", 64, 65), R("bo32"), R("acc", 0, 1))])
            act(R("a16", 0, 1), R("p5", 64, 65), bias=130 - 7.5 / 16, scale=1.0 / 16)
            act(R("nthr", 1, 2), R("p5", 64, 65), bias=col(cNT6), scale=-1.0)
            act(R("nthr", 0, 1), R("a16", 0, 1), bias=R("nthr", 1, 2), scale=16.0)
    mm(wrap(R("p2", 0, 128), "wd", lambda s: R("xw", F0 + 128 * s, F0 + 128 + 128 * s)))
    act(R("yff"), R("p2", 0, 128), bias=1024.0)
    dma("S", "yf", ("h", "yf"), R("yff"))
    return ops


def depend(ops):
    seen = {}
    for i, o in enumerate(ops):
        hard, soft = set(), set()
        if o["kind"] == "arrive":
            soft.add(i - 1)
        else:
            for x, isw in [(x, False) for x in o["r"]] + [(x, True) for x in o["w"]]:
                for j, y, yw in seen.get(x[1], []):
                    if y & x[4] and (isw or yw):
                        (soft if o["eng"] == ops[j]["eng"] == "P" else hard).add(j)
        if o["kind"] != "mm":
            for x in o["w"]:
                if x[3] is None:
                    seen[x[1]] = [e for e in seen.get(x[1], []) if e[1] & ~x[4]]
        for lst, isw in ((o["r"], False), (o["w"], True)):
            both = {}
            for x in lst:
                both[x[1]] = both.get(x[1], 0) | x[4]
            for n, bits in both.items():
                seen.setdefault(n, []).append((i, bits, isw))
        o["data"], o["soft"] = hard, soft - hard
        o["banks"] = sorted(set(x[1] for x in o["r"] + o["w"] if SCRATCH[x[1]][0] == "psum"))
    return ops


def arrange(ops):
    key = [(o["visit"] or 0) + WHEN[("i" if o["visit"] is None else "") + o["nth"]] for o in ops]
    left, after = [len(o["data"] | o["soft"]) for o in ops], [[] for _ in ops]
    for i, o in enumerate(ops):
        for j in o["data"] | o["soft"]:
            after[j].append(i)
    ready, order, bank = [(key[i], i) for i in range(len(ops)) if not left[i]], [], {}
    while ready:
        ready.sort(reverse=True)
        i = ready.pop()[1]
        order.append(i)
        o = ops[i]
        o["hard"] = set(o["data"])
        for b in o["banks"]:
            o["hard"] |= set(j for e, j in bank.setdefault(b, {}).items() if e != o["eng"])
            bank[b][o["eng"]] = i
        for k in after[i]:
            left[k] -= 1
            if not left[k]:
                ready.append((key[k], k))
    return order


PLAN = []


def rank_program(g, core, T, topo):
    rank = T.rank_of(core)
    if rank is None:
        return
    if not PLAN:
        PLAN.append(depend(build()))
        PLAN.append(arrange(PLAN[0]))
    ops, order = PLAN
    Q = {"V": g.vector, "S": g.scalar, "P": g.tensor, "G": g, "Y": g.sync}

    def ap(x):
        if not isinstance(x, tuple):
            return x
        if x[0] == "h":
            return T[x[1]][:]
        if x[0] == "i":
            return ap(x[1]).indirect(ap(x[2]))
        return T[x[1]][(ALL if x[3] is None else slice(x[3][0], x[3][1]),) + x[2]]

    def route(v):
        s = 1 + v % (N - 1)
        return T.cores[(rank + s) % N], T.cores[(rank - s) % N]

    pos, known, clock, waits = {i: p for p, i in enumerate(order)}, {e: {} for e in Q}, {}, {}
    for i in order:
        o = ops[i]
        e = o["eng"]
        line = i if o["kind"] in ("dma", "arrive") else e
        if o["kind"] == "arrive":
            clock[i] = {line: pos[i]}
            continue
        waits[i] = []
        for j in sorted(o["hard"], key=lambda j: -pos[j]):
            lj = j if ops[j]["kind"] in ("dma", "arrive") else ops[j]["eng"]
            if ops[j]["kind"] != "send" and known[e].get(lj, -1) < pos[j]:
                waits[i].append(j)
                for key, p in clock[j].items():
                    known[e][key] = max(known[e].get(key, -1), p)
        clock[i] = dict(known[e])
        clock[i][line] = pos[i]
    needed = set(j for w in waits.values() for j in w)
    token, count = {}, {e: 0 for e in "VSPG"}
    sent = 0
    for i in order:
        o = ops[i]
        e, kind, a = o["eng"], o["kind"], o["args"]
        if kind == "arrive":
            token[i] = (a, len(topo.engines(route(int(a[2:]) - 1)[1], core)))
            continue
        q = Q[e]
        for j in waits[i]:
            q.wait_ge(T.sem[token[j][0]], token[j][1])
        if kind == "dma":
            q.dma_start(ap(a[1]), ap(a[2])).then_inc(T.sem["d_" + a[0]], 16)
            token[i] = ("d_" + a[0], 16)
            continue
        if kind == "send":
            v = a[1]
            dst = route(v)[0]
            rid, pid = topo.addr(dst, core)
            if a[0] == "L":
                src, out = T.ls[:, v * K:v * K + K], T.lu[:, (v + 1) * K:(v + 2) * K]
            else:
                src, out = T.zo[:, v * K:v * K + K], T.zb[:, (v + 1) * K:(v + 2) * K]
            g.remote_dma(out, src, T.sem["a%s%d" % (a[0], v + 1)], T.sem.sent, pid, rid, topo.mask(core, dst))
            sent += len(topo.engines(core, dst))
            continue
        if kind == "copy":
            ins = q.tensor_copy(ap(a[0]), ap(a[1]))
        elif kind == "tt":
            ins = q.tensor_tensor(ap(a[0]), ap(a[1]), ap(a[2]), a[3])
        elif kind == "ts":
            if a[5] is None:
                ins = q.tensor_scalar(ap(a[0]), ap(a[1]), ap(a[2]), None, a[4])
            else:
                ins = q.tensor_scalar(ap(a[0]), ap(a[1]), ap(a[2]), ap(a[3]), a[4], a[5])
        elif kind == "scan":
            ins = q.tensor_tensor_scan(ap(a[0]), ap(a[1]), ap(a[2]), 0.0, ALU.min, ALU.max)
        elif kind == "ms":
            ins = q.memset(ap(a[0]), a[1])
        elif kind == "act" and a[0][0] == "i":
            ins = q.activation(ap(a[0]), ap(a[1]), a[2])
        elif kind == "act":
            ins = q.activation(ap(a[0]), ap(a[1]), a[2], bias=ap(a[3]), scale=ap(a[4]), accum_out=ap(a[5]))
        elif kind == "mm":
            start, stop, each = o["group"]
            for m, (out, l, r) in enumerate(a):
                ins = q.matmul(ap(out), ap(l), ap(r), each or (start and m == 0), each or (stop and m == len(a) - 1))
        elif kind == "iota":
            if SCRATCH[a[0][1]][2] == "int32":
                ins = q.iota(ap(a[0]), a[1], a[2], a[3])
            else:
                ins = q.iota(ap(a[0]), a[1], a[2], a[3], allow_small_or_imprecise_dtypes=True)
        else:
            ins = q.affine_select(ap(a[0]), ap(a[1]), a[2], a[3], a[4], a[5], a[6])
        if i in needed:
            count[e] += 1
            ins.then_inc(T.sem["e" + e], 1)
            token[i] = ("e" + e, count[e])
    for e in "VSPG":
        g.sync.wait_ge(T.sem["e" + e], count[e])
    for n in DMAS:
        g.sync.wait_ge(T.sem["d_" + n], 16)
    g.wait_ge(T.sem.sent, sent)
